import numpy as np
import ml_dtypes


def mxq(x, axis, fmt="e4m3"):
    dtype, down = {"e4m3": (ml_dtypes.float8_e4m3fn, 7), "e5m2": (ml_dtypes.float8_e5m2, 14)}[fmt]
    v = np.moveaxis(np.asarray(x, np.float32).astype(ml_dtypes.bfloat16).astype(np.float64), axis, -1)
    blocks = v.reshape(v.shape[:-1] + (-1, 32))
    amax = np.abs(blocks).max(-1, keepdims=True)
    byte = np.maximum(np.where(amax > 0, np.frexp(amax)[1] - 1 + 127, 0) - down, 1)
    scale = np.exp2(byte - 127.0)
    codes = (blocks / scale).astype(np.float32).astype(dtype).astype(np.float64)
    return np.moveaxis((codes * scale).reshape(v.shape), -1, axis)


WIDE = False


def mx_kscale(k):
    if not WIDE:
        return np.ones(k)
    levels = np.array([10, -10, 5, -5, 0])
    if k % 512:
        return np.exp2(np.random.permutation(np.resize(levels, k // 32))).repeat(32)
    a = np.empty((k // 512, 16))
    for p in range(k // 512):
        a[p, :8] = np.random.permutation(np.resize(levels, 8))
        for g in range(8):
            far = levels[np.abs(levels - a[p, g]) >= 10]
            a[p, g + 8] = far[np.random.randint(len(far))]
    return np.exp2(a.ravel()).repeat(32)


def f64(x):
    return np.asarray(x).astype(np.float64)


def striped(idx):
    return np.tile(np.asarray(idx).reshape(-1, 16).T, (8, 1)).astype(np.uint16)


def unstriped(offs):
    return offs[:16].T.reshape(-1).astype(np.int64)


E2M1 = np.array([0.0, 0.5, 1.0, 1.5, 2.0, 3.0, 4.0, 6.0, -0.0, -0.5, -1.0, -1.5, -2.0, -3.0, -4.0, -6.0])


def pack_weight(w, fmt):
    k, n = w.shape
    w = f64(np.asarray(w, np.float32).astype(ml_dtypes.bfloat16)).reshape(k // 32, 32, n)
    amax = np.abs(w).max(1)
    if fmt == "e4m3":
        byte = np.frexp(amax)[1] - 1 + 127 - 7
    else:
        mant, ex = np.frexp(amax / 6.0)
        byte = np.where(mant > 0.5, ex, ex - 1) + 127
    byte = np.clip(np.where(amax > 0, byte, 1), 1, 254)
    scaled = (w * np.exp2(127.0 - byte)[:, None, :]).reshape(k, n).astype(np.float32)
    by_word = np.ascontiguousarray(scaled.reshape(k // 512, 128, 4, n).transpose(0, 1, 3, 2))
    if fmt == "e4m3":
        words = by_word.astype(ml_dtypes.float8_e4m3fn).view(np.uint8)
    else:
        c = by_word.astype(ml_dtypes.float4_e2m1fn).view(np.uint8) & 0xF
        words = (c[..., 0::2] | (c[..., 1::2] << 4)).reshape(k // 512, 128, 2 * n)
    return np.ascontiguousarray(words), np.ascontiguousarray(byte.astype(np.uint8).reshape(k // 512, 16, n))


def unpack_weight(words, scales, fmt):
    g, _, n = scales.shape
    words = np.ascontiguousarray(words).reshape(g, 128, n, -1)
    if fmt == "e4m3":
        vals = words.view(ml_dtypes.float8_e4m3fn).astype(np.float64)
    else:
        nib = np.empty((g, 128, n, 4), np.uint8)
        nib[..., 0::2] = words & 0xF
        nib[..., 1::2] = words >> 4
        vals = E2M1[nib]
    vals = vals * np.repeat(np.exp2(scales.astype(np.float64) - 127.0), 8, axis=1)[..., None]
    return vals.transpose(0, 1, 3, 2).reshape(g * 512, n)


B, N, T, D, DV, NQ = 1, 512, 1024, 1536, 0, 256


def setup_inputs():
    n = np.random.standard_normal
    idx = np.sort(np.random.permutation(T)[:B * N].reshape(B, N), axis=1).reshape(-1)
    s = mx_kscale(D)[:, None]
    r = np.random.uniform(0.5, 2.0, T)
    kp = pack_weight(n((D, T)) / s / r, "e4m3")
    return {
        "qT": (n((B, D, NQ)) * s * (1.00 / np.sqrt(D))).astype(np.float32),
        "k_words": kp[0],
        "k_scales": kp[1],
        "ts": np.tile(r, (128, 1)).astype(np.float32),
        "offs": striped(idx),
    }


def reference(qT, k_words, k_scales, ts, offs):
    idx = unstriped(offs)
    pool = unpack_weight(k_words, k_scales, "e4m3")
    pick = lambda x: x[:, idx].reshape(x.shape[0], B, N).transpose(1, 0, 2)
    a = mxq(f64(qT), 1, "e4m3").transpose(0, 2, 1) @ pick(pool)
    a = a * pick(f64(ts))[:, :1, :]
    out = np.zeros((B, NQ, T))
    for b in range(B):
        out[b][:, idx[b * N:(b + 1) * N]] = a[b]
    return out

@@ -1,0 +1,146 @@
+from contextlib import ExitStack
+
+import concourse.mybir as mybir
+from concourse.masks import make_identity
+
+NQ, N, T, D = 256, 512, 1024, 1536
+FLOPS = 2 * NQ * N * D
+
+F32 = mybir.dt.float32
+BF16 = mybir.dt.bfloat16
+I32 = mybir.dt.int32
+U32 = mybir.dt.uint32
+U16 = mybir.dt.uint16
+U8 = mybir.dt.uint8
+FP8X4 = mybir.dt.float8_e4m3fn_x4
+MULT = mybir.AluOpType.mult
+
+P = 128
+PACK = 4
+K_PASS = P * PACK
+PASSES = D // K_PASS
+BLOCKS = NQ // P
+HALVES = 2
+HALF = N // HALVES
+LIST_COLS = N // 16
+TS_PER_PART = T // P
+ODD = T // 2 + 1
+
+
+def tile_attend_sddmm_ts_srt_kernel(tc, qT, k_words, k_scales, ts, offs, out):
+    nc = tc.nc
+    with ExitStack() as ctx:
+        keep = ctx.enter_context(tc.tile_pool(name="keep", bufs=1))
+        reuse = ctx.enter_context(tc.tile_pool(name="reuse", bufs=1))
+        psum = ctx.enter_context(tc.psum_pool(name="psum", bufs=1))
+
+        offsets = keep.tile([P, LIST_COLS], U16, name="offsets")
+        ts_row = keep.tile([P, TS_PER_PART], F32, name="ts_row")
+        q_raw = [keep.tile([P, PACK, NQ], F32, name=f"q_raw{o}") for o in range(PASSES)]
+        pool_words = [keep.tile([P, T], U32, name=f"pool_words{o}", align_bytes=64) for o in range(PASSES)]
+        pool_scales = reuse.tile([P, T], U8, name="pool_scales", align_bytes=64, offset=1984)
+        ident = keep.tile([P, P], F32, name="ident")
+        warm = keep.tile([P, 8], F32, name="warm")
+        warm2 = keep.tile([P, 8], F32, name="warm2")
+
+        def load_q(o):
+            nc.sync.dma_start(out=q_raw[o][:], in_=qT[0, o * K_PASS:(o + 1) * K_PASS, :].rearrange("(p j) w -> p j w", j=PACK))
+
+        nc.gpsimd.memset(pool_scales[:].bitcast(I32), 0)
+        nc.vector.memset(warm[:], 0.0)
+        nc.scalar.copy(out=warm2[:], in_=warm[:])
+        make_identity(nc, ident[:])
+        load_q(0)
+        nc.sync.dma_start(out=ts_row[:], in_=ts[0].rearrange("(k m) -> k m", m=TS_PER_PART))
+        nc.sync.dma_start(offsets[:], offs)
+        for o in range(PASSES):
+            if o > 0:
+                load_q(o)
+            nc.sync.dma_start(out=pool_words[o][:].bitcast(I32), in_=k_words[o].rearrange("p t r -> p (t r)").bitcast(I32))
+        for quad in range(4):
+            nc.gpsimd.dma_start(out=pool_scales[32 * quad:32 * quad + 4 * PASSES, :].bitcast(I32),
+                                in_=k_scales[:, 4 * quad:4 * quad + 4, :].bitcast(I32))
+
+        rows = [keep.tile([P, T], F32, name=f"rows{b}") for b in range(BLOCKS)]
+        for b in range(BLOCKS):
+            nc.vector.memset(rows[b][:, :ODD], 0.0)
+            nc.vector.memset(rows[b][:, ODD:], 0.0)
+
+        ts_pool = keep.tile([P, T], F32, name="ts_pool")
+        for g in range(2):
+            spread = psum.tile([P, 4, P], F32, name=f"spread{g}")
+            for m in range(4):
+                col = 4 * g + m
+                nc.tensor.transpose(spread[:, m, :], ts_row[:, col:col + 1].to_broadcast([P, P]), ident[:])
+            nc.scalar.copy(out=ts_pool[:].rearrange("p (k g m) -> p k g m", g=2, m=4)[:, :, g, :],
+                           in_=spread[:].rearrange("p m k -> p k m"))
+
+        q_grouped = [keep.tile([P, NQ, PACK], BF16, name=f"q_grouped{o}", align_bytes=64) for o in range(PASSES)]
+        q_codes = [keep.tile([P, NQ], U32, name=f"q_codes{o}", align_bytes=64) for o in range(PASSES)]
+        q_scales = [keep.tile([P, NQ], U8, name="q_scales0", align_bytes=64),
+                    reuse.tile([P, NQ], U8, name="q_scales1", align_bytes=64, offset=2048),
+                    reuse.tile([P, NQ], U8, name="q_scales2", align_bytes=64, offset=2304)]
+
+        def interleave(o, cols):
+            src = q_raw[o][:, :, cols].rearrange("p j w -> p w j")
+            if o == 0:
+                nc.vector.tensor_copy(out=q_grouped[o][:, cols, :], in_=src)
+            else:
+                nc.scalar.copy(out=q_grouped[o][:, cols, :], in_=src)
+
+        def quantize(o, cols):
+            nc.vector.quantize_mx(out=q_codes[o][:, cols].bitcast(FP8X4), scales=q_scales[o][:, cols],
+                                  in_=q_grouped[o][:, cols, :].rearrange("p w j -> p (w j)"))
+
+        def block(b):
+            return slice(b * P, (b + 1) * P)
+
+        key_words = [keep.tile([P, N], U32, name="key_words0", align_bytes=64),
+                     reuse.tile([P, N], U32, name="key_words1", align_bytes=64, offset=0),
+                     reuse.tile([P, N], U32, name="key_words2", align_bytes=64, offset=2944)]
+        key_scales = keep.tile([P, N], U8, name="key_scales", align_bytes=64)
+        ts_listed = keep.tile([P, N], F32, name="ts_listed")
+        acc = [[psum.tile([P, HALF], F32, name=f"acc{b}{h}") for h in range(HALVES)] for b in range(BLOCKS)]
+        scores = [[keep.tile([P, HALF], F32, name=f"scores{b}{h}") for h in range(HALVES)] for b in range(BLOCKS)]
+
+        def slots(h):
+            return slice(h * HALF, (h + 1) * HALF)
+
+        def entries(h):
+            return offsets[:, h * HALF // 16:(h + 1) * HALF // 16]
+
+        def multiply(o, b, h):
+            cols = slice(b * P, (b + 1) * P)
+            nc.tensor.matmul_mx(out=acc[b][h][:], lhsT=q_codes[o][:, cols].bitcast(FP8X4), lhsT_scale=q_scales[o][:, cols],
+                                rhs=key_words[o][:, slots(h)].bitcast(FP8X4), rhs_scale=key_scales[4 * o:P, slots(h)],
+                                start=(o == 0), stop=(o == PASSES - 1))
+
+        every = slice(0, NQ)
+        last = PASSES - 1
+        for o in range(last):
+            interleave(o, every)
+        for b in range(BLOCKS):
+            interleave(last, block(b))
+        nc.vector.tensor_copy(out=key_words[0][:], in_=pool_words[0][:].indirect(offsets[:]))
+        quantize(0, every)
+        nc.vector.tensor_copy(out=ts_listed[:], in_=ts_pool[:].indirect(offsets[:]))
+        nc.vector.tensor_copy(out=key_scales[:], in_=pool_scales[:].indirect(offsets[:]))
+        nc.vector.tensor_copy(out=key_words[1][:], in_=pool_words[1][:].indirect(offsets[:]))
+        quantize(1, every)
+        for o in range(last):
+            for b in range(BLOCKS):
+                for h in range(HALVES):
+                    multiply(o, b, h)
+        for h in range(HALVES):
+            quantize(last, block(h))
+            nc.vector.tensor_copy(out=key_words[last][:, slots(h)], in_=pool_words[last][:].indirect(entries(h)))
+        for b in range(BLOCKS):
+            for h in range(HALVES):
+                multiply(last, b, h)
+        for b in range(BLOCKS):
+            for h in range(HALVES):
+                nc.scalar.copy(out=scores[b][h][:], in_=acc[b][h][:])
+        for b in range(BLOCKS):
+            for h in range(HALVES):
+                nc.vector.tensor_tensor(rows[b][:].indirect(entries(h)), scores[b][h][:], ts_listed[:, slots(h)], MULT)
+            nc.sync.dma_start(out=out[0, b * P:(b + 1) * P, :], in_=rows[b][:])

@@ -31,40 +31,46 @@ def tile_attend_sddmm_ts_srt_kernel(tc, qT, k_words, k_scales, ts, offs, out):
     nc = tc.nc
     with ExitStack() as ctx:
         keep = ctx.enter_context(tc.tile_pool(name="keep", bufs=1))
-        reuse = ctx.enter_context(tc.tile_pool(name="reuse", bufs=1))
         psum = ctx.enter_context(tc.psum_pool(name="psum", bufs=1))
 
         offsets = keep.tile([P, LIST_COLS], U16, name="offsets")
         ts_row = keep.tile([P, TS_PER_PART], F32, name="ts_row")
         q_raw = [keep.tile([P, PACK, NQ], F32, name=f"q_raw{o}") for o in range(PASSES)]
         pool_words = [keep.tile([P, T], U32, name=f"pool_words{o}", align_bytes=64) for o in range(PASSES)]
-        pool_scales = reuse.tile([P, T], U8, name="pool_scales", align_bytes=64, offset=1984)
+        pool_scales = keep.tile([P, T], U8, name="pool_scales", align_bytes=64)
         ident = keep.tile([P, P], F32, name="ident")
         warm = keep.tile([P, 8], F32, name="warm")
         warm2 = keep.tile([P, 8], F32, name="warm2")
 
-        def load_q(o):
-            nc.sync.dma_start(out=q_raw[o][:], in_=qT[0, o * K_PASS:(o + 1) * K_PASS, :].rearrange("(p j) w -> p j w", j=PACK))
+        def block(b):
+            return slice(b * P, (b + 1) * P)
+
+        def load_q(o, cols):
+            nc.sync.dma_start(out=q_raw[o][:, :, cols],
+                              in_=qT[0, o * K_PASS:(o + 1) * K_PASS, cols].rearrange("(p j) w -> p j w", j=PACK))
+
+        def load_words(o):
+            nc.sync.dma_start(out=pool_words[o][:].bitcast(I32), in_=k_words[o].rearrange("p t r -> p (t r)").bitcast(I32))
 
         nc.gpsimd.memset(pool_scales[:].bitcast(I32), 0)
+        make_identity(nc, ident[:])
         nc.vector.memset(warm[:], 0.0)
         nc.scalar.copy(out=warm2[:], in_=warm[:])
-        make_identity(nc, ident[:])
-        load_q(0)
-        nc.sync.dma_start(out=ts_row[:], in_=ts[0].rearrange("(k m) -> k m", m=TS_PER_PART))
+        load_words(0)
         nc.sync.dma_start(offsets[:], offs)
-        for o in range(PASSES):
-            if o > 0:
-                load_q(o)
-            nc.sync.dma_start(out=pool_words[o][:].bitcast(I32), in_=k_words[o].rearrange("p t r -> p (t r)").bitcast(I32))
+        nc.sync.dma_start(out=ts_row[:], in_=ts[0].rearrange("(k m) -> k m", m=TS_PER_PART))
+        load_words(1)
+        load_words(2)
         for quad in range(4):
-            nc.gpsimd.dma_start(out=pool_scales[32 * quad:32 * quad + 4 * PASSES, :].bitcast(I32),
-                                in_=k_scales[:, 4 * quad:4 * quad + 4, :].bitcast(I32))
+            nc.sync.dma_start(out=pool_scales[32 * quad:32 * quad + 4 * PASSES, :].bitcast(I32),
+                              in_=k_scales[:, 4 * quad:4 * quad + 4, :].bitcast(I32))
+        for b in range(BLOCKS):
+            for o in range(PASSES):
+                load_q(o, block(b))
 
         rows = [keep.tile([P, T], F32, name=f"rows{b}") for b in range(BLOCKS)]
         for b in range(BLOCKS):
-            nc.vector.memset(rows[b][:, :ODD], 0.0)
-            nc.vector.memset(rows[b][:, ODD:], 0.0)
+            nc.vector.memset(rows[b][:], 0.0)
 
         ts_pool = keep.tile([P, T], F32, name="ts_pool")
         for g in range(2):
@@ -78,26 +84,20 @@ def tile_attend_sddmm_ts_srt_kernel(tc, qT, k_words, k_scales, ts, offs, out):
         q_grouped = [keep.tile([P, NQ, PACK], BF16, name=f"q_grouped{o}", align_bytes=64) for o in range(PASSES)]
         q_codes = [keep.tile([P, NQ], U32, name=f"q_codes{o}", align_bytes=64) for o in range(PASSES)]
         q_scales = [keep.tile([P, NQ], U8, name="q_scales0", align_bytes=64),
-                    reuse.tile([P, NQ], U8, name="q_scales1", align_bytes=64, offset=2048),
-                    reuse.tile([P, NQ], U8, name="q_scales2", align_bytes=64, offset=2304)]
+                    keep.tile([P, NQ], U8, name="q_scales1", align_bytes=64),
+                    keep.tile([P, NQ], U8, name="q_scales2", align_bytes=64)]
 
         def interleave(o, cols):
-            src = q_raw[o][:, :, cols].rearrange("p j w -> p w j")
-            if o == 0:
-                nc.vector.tensor_copy(out=q_grouped[o][:, cols, :], in_=src)
-            else:
-                nc.scalar.copy(out=q_grouped[o][:, cols, :], in_=src)
+            nc.scalar.copy(out=q_grouped[o][:, cols, :].rearrange("p (c i) j -> p c j i", i=4),
+                           in_=q_raw[o][:, :, cols].rearrange("p j (c i) -> p c j i", i=4))
 
         def quantize(o, cols):
             nc.vector.quantize_mx(out=q_codes[o][:, cols].bitcast(FP8X4), scales=q_scales[o][:, cols],
                                   in_=q_grouped[o][:, cols, :].rearrange("p w j -> p (w j)"))
 
-        def block(b):
-            return slice(b * P, (b + 1) * P)
-
         key_words = [keep.tile([P, N], U32, name="key_words0", align_bytes=64),
-                     reuse.tile([P, N], U32, name="key_words1", align_bytes=64, offset=0),
-                     reuse.tile([P, N], U32, name="key_words2", align_bytes=64, offset=2944)]
+                     keep.tile([P, N], U32, name="key_words1", align_bytes=64),
+                     keep.tile([P, N], U32, name="key_words2", align_bytes=64)]
         key_scales = keep.tile([P, N], U8, name="key_scales", align_bytes=64)
         ts_listed = keep.tile([P, N], F32, name="ts_listed")
         acc = [[psum.tile([P, HALF], F32, name=f"acc{b}{h}") for h in range(HALVES)] for b in range(BLOCKS)]
@@ -115,32 +115,23 @@ def tile_attend_sddmm_ts_srt_kernel(tc, qT, k_words, k_scales, ts, offs, out):
                                 rhs=key_words[o][:, slots(h)].bitcast(FP8X4), rhs_scale=key_scales[4 * o:P, slots(h)],
                                 start=(o == 0), stop=(o == PASSES - 1))
 
-        every = slice(0, NQ)
-        last = PASSES - 1
-        for o in range(last):
-            interleave(o, every)
-        for b in range(BLOCKS):
-            interleave(last, block(b))
-        nc.vector.tensor_copy(out=key_words[0][:], in_=pool_words[0][:].indirect(offsets[:]))
-        quantize(0, every)
-        nc.vector.tensor_copy(out=ts_listed[:], in_=ts_pool[:].indirect(offsets[:]))
+        def scatter(b, h):
+            nc.vector.tensor_tensor(rows[b][:].indirect(entries(h)), scores[b][h][:], ts_listed[:, slots(h)], MULT)
+
+        for o in range(PASSES):
+            nc.vector.tensor_copy(out=key_words[o][:], in_=pool_words[o][:].indirect(offsets[:]))
         nc.vector.tensor_copy(out=key_scales[:], in_=pool_scales[:].indirect(offsets[:]))
-        nc.vector.tensor_copy(out=key_words[1][:], in_=pool_words[1][:].indirect(offsets[:]))
-        quantize(1, every)
-        for o in range(last):
-            for b in range(BLOCKS):
+        nc.vector.tensor_copy(out=ts_listed[:], in_=ts_pool[:].indirect(offsets[:]))
+        for b in range(BLOCKS):
+            for o in range(PASSES):
+                interleave(o, block(b))
+                quantize(o, block(b))
+            for o in range(PASSES):
                 for h in range(HALVES):
                     multiply(o, b, h)
-        for h in range(HALVES):
-            quantize(last, block(h))
-            nc.vector.tensor_copy(out=key_words[last][:, slots(h)], in_=pool_words[last][:].indirect(entries(h)))
-        for b in range(BLOCKS):
-            for h in range(HALVES):
-                multiply(last, b, h)
-        for b in range(BLOCKS):
             for h in range(HALVES):
                 nc.scalar.copy(out=scores[b][h][:], in_=acc[b][h][:])
         for b in range(BLOCKS):
             for h in range(HALVES):
-                nc.vector.tensor_tensor(rows[b][:].indirect(entries(h)), scores[b][h][:], ts_listed[:, slots(h)], MULT)
+                scatter(b, h)
             nc.sync.dma_start(out=out[0, b * P:(b + 1) * P, :], in_=rows[b][:])

@@ -36,7 +36,7 @@ def tile_attend_sddmm_ts_srt_kernel(tc, qT, k_words, k_scales, ts, offs, out):
         offsets = keep.tile([P, LIST_COLS], U16, name="offsets")
         ts_row = keep.tile([P, TS_PER_PART], F32, name="ts_row")
         q_raw = [keep.tile([P, PACK, NQ], F32, name=f"q_raw{o}") for o in range(PASSES)]
-        pool_words = [keep.tile([P, T], U32, name=f"pool_words{o}", align_bytes=64) for o in range(PASSES)]
+        pool_words = [keep.tile([P, T], U32, name=f"pool_words{o}") for o in range(PASSES)]
         pool_scales = keep.tile([P, T], U8, name="pool_scales", align_bytes=64)
         ident = keep.tile([P, P], F32, name="ident")
         warm = keep.tile([P, 8], F32, name="warm")
@@ -53,20 +53,21 @@ def tile_attend_sddmm_ts_srt_kernel(tc, qT, k_words, k_scales, ts, offs, out):
             nc.sync.dma_start(out=pool_words[o][:].bitcast(I32), in_=k_words[o].rearrange("p t r -> p (t r)").bitcast(I32))
 
         nc.gpsimd.memset(pool_scales[:].bitcast(I32), 0)
-        make_identity(nc, ident[:])
-        nc.vector.memset(warm[:], 0.0)
+        nc.gpsimd.memset(warm[:], 0.0)
         nc.scalar.copy(out=warm2[:], in_=warm[:])
+        make_identity(nc, ident[:])
         load_words(0)
         nc.sync.dma_start(offsets[:], offs)
         nc.sync.dma_start(out=ts_row[:], in_=ts[0].rearrange("(k m) -> k m", m=TS_PER_PART))
+        load_q(0, slice(0, NQ))
         load_words(1)
-        load_words(2)
         for quad in range(4):
             nc.sync.dma_start(out=pool_scales[32 * quad:32 * quad + 4 * PASSES, :].bitcast(I32),
                               in_=k_scales[:, 4 * quad:4 * quad + 4, :].bitcast(I32))
-        for b in range(BLOCKS):
-            for o in range(PASSES):
-                load_q(o, block(b))
+        load_q(1, slice(0, NQ))
+        load_q(2, block(0))
+        load_words(2)
+        load_q(2, block(1))
 
         rows = [keep.tile([P, T], F32, name=f"rows{b}") for b in range(BLOCKS)]
         for b in range(BLOCKS):
@@ -81,57 +82,52 @@ def tile_attend_sddmm_ts_srt_kernel(tc, qT, k_words, k_scales, ts, offs, out):
             nc.scalar.copy(out=ts_pool[:].rearrange("p (k g m) -> p k g m", g=2, m=4)[:, :, g, :],
                            in_=spread[:].rearrange("p m k -> p k m"))
 
-        q_grouped = [keep.tile([P, NQ, PACK], BF16, name=f"q_grouped{o}", align_bytes=64) for o in range(PASSES)]
         q_codes = [keep.tile([P, NQ], U32, name=f"q_codes{o}", align_bytes=64) for o in range(PASSES)]
-        q_scales = [keep.tile([P, NQ], U8, name="q_scales0", align_bytes=64),
-                    keep.tile([P, NQ], U8, name="q_scales1", align_bytes=64),
-                    keep.tile([P, NQ], U8, name="q_scales2", align_bytes=64)]
+        q_scales = [keep.tile([P, NQ], U8, name=f"q_scales{o}", align_bytes=64) for o in range(PASSES)]
 
-        def interleave(o, cols):
-            nc.scalar.copy(out=q_grouped[o][:, cols, :].rearrange("p (c i) j -> p c j i", i=4),
+        def quantize(o, cols, tag):
+            width = cols.stop - cols.start
+            grouped = keep.tile([P, width, PACK], BF16, name="grouped", tag=tag, align_bytes=64)
+            nc.scalar.copy(out=grouped[:].rearrange("p (c i) j -> p c j i", i=4),
                            in_=q_raw[o][:, :, cols].rearrange("p j (c i) -> p c j i", i=4))
-
-        def quantize(o, cols):
             nc.vector.quantize_mx(out=q_codes[o][:, cols].bitcast(FP8X4), scales=q_scales[o][:, cols],
-                                  in_=q_grouped[o][:, cols, :].rearrange("p w j -> p (w j)"))
+                                  in_=grouped[:].rearrange("p w j -> p (w j)"))
 
-        key_words = [keep.tile([P, N], U32, name="key_words0", align_bytes=64),
-                     keep.tile([P, N], U32, name="key_words1", align_bytes=64),
-                     keep.tile([P, N], U32, name="key_words2", align_bytes=64)]
+        key_words = [keep.tile([P, N], U32, name=f"key_words{o}", align_bytes=64) for o in range(PASSES)]
         key_scales = keep.tile([P, N], U8, name="key_scales", align_bytes=64)
-        ts_listed = keep.tile([P, N], F32, name="ts_listed")
-        acc = [[psum.tile([P, HALF], F32, name=f"acc{b}{h}") for h in range(HALVES)] for b in range(BLOCKS)]
-        scores = [[keep.tile([P, HALF], F32, name=f"scores{b}{h}") for h in range(HALVES)] for b in range(BLOCKS)]
+        parts = [(0, 0, HALF), (0, HALF, HALF), (1, 0, N)]
+        acc = [psum.tile([P, n], F32, name=f"acc{b}_{s0}") for b, s0, n in parts]
+        scores = [keep.tile([P, n], F32, name=f"scores{b}_{s0}") for b, s0, n in parts]
 
-        def slots(h):
-            return slice(h * HALF, (h + 1) * HALF)
-
-        def entries(h):
-            return offsets[:, h * HALF // 16:(h + 1) * HALF // 16]
-
-        def multiply(o, b, h):
-            cols = slice(b * P, (b + 1) * P)
-            nc.tensor.matmul_mx(out=acc[b][h][:], lhsT=q_codes[o][:, cols].bitcast(FP8X4), lhsT_scale=q_scales[o][:, cols],
-                                rhs=key_words[o][:, slots(h)].bitcast(FP8X4), rhs_scale=key_scales[4 * o:P, slots(h)],
+        def multiply(o, i):
+            b, s0, n = parts[i]
+            nc.tensor.matmul_mx(out=acc[i][:], lhsT=q_codes[o][:, block(b)].bitcast(FP8X4), lhsT_scale=q_scales[o][:, block(b)],
+                                rhs=key_words[o][:, s0:s0 + n].bitcast(FP8X4), rhs_scale=key_scales[4 * o:P, s0:s0 + n],
                                 start=(o == 0), stop=(o == PASSES - 1))
 
-        def scatter(b, h):
-            nc.vector.tensor_tensor(rows[b][:].indirect(entries(h)), scores[b][h][:], ts_listed[:, slots(h)], MULT)
+        def gather_words(o, s0, n):
+            nc.vector.tensor_copy(out=key_words[o][:, s0:s0 + n],
+                                  in_=pool_words[o][:].indirect(offsets[:, s0 // 16:(s0 + n) // 16]))
 
-        for o in range(PASSES):
-            nc.vector.tensor_copy(out=key_words[o][:], in_=pool_words[o][:].indirect(offsets[:]))
+        last = PASSES - 1
+        ts_listed = keep.tile([P, N], F32, name="ts_listed")
         nc.vector.tensor_copy(out=key_scales[:], in_=pool_scales[:].indirect(offsets[:]))
+        for o in range(last):
+            gather_words(o, 0, N)
+            quantize(o, slice(0, NQ), f"grouped{o}")
+            for i in range(len(parts)):
+                multiply(o, i)
+        quantize(last, block(0), "grouped_a")
         nc.vector.tensor_copy(out=ts_listed[:], in_=ts_pool[:].indirect(offsets[:]))
-        for b in range(BLOCKS):
-            for o in range(PASSES):
-                interleave(o, block(b))
-                quantize(o, block(b))
-            for o in range(PASSES):
-                for h in range(HALVES):
-                    multiply(o, b, h)
-            for h in range(HALVES):
-                nc.scalar.copy(out=scores[b][h][:], in_=acc[b][h][:])
-        for b in range(BLOCKS):
-            for h in range(HALVES):
-                scatter(b, h)
-            nc.sync.dma_start(out=out[0, b * P:(b + 1) * P, :], in_=rows[b][:])
+        for i in range(2):
+            gather_words(last, i * HALF, HALF)
+            multiply(last, i)
+            nc.scalar.copy(out=scores[i][:], in_=acc[i][:])
+        quantize(last, block(1), "grouped_b")
+        multiply(last, 2)
+        nc.scalar.copy(out=scores[2][:], in_=acc[2][:])
+        for i, (b, s0, n) in enumerate(parts):
+            nc.vector.tensor_tensor(rows[b][:].indirect(offsets[:, s0 // 16:(s0 + n) // 16]), scores[i][:],
+                                    ts_listed[:, s0:s0 + n], MULT)
+            if s0 + n == N:
+                nc.sync.dma_start(out=out[0, block(b), :], in_=rows[b][:])

@@ -24,7 +24,7 @@ HALVES = 2
 HALF = N // HALVES
 LIST_COLS = N // 16
 TS_PER_PART = T // P
-ODD = T // 2 + 1
+REACH = T - N + HALF
 
 
 def tile_attend_sddmm_ts_srt_kernel(tc, qT, k_words, k_scales, ts, offs, out):
@@ -49,25 +49,27 @@ def tile_attend_sddmm_ts_srt_kernel(tc, qT, k_words, k_scales, ts, offs, out):
             nc.sync.dma_start(out=q_raw[o][:, :, cols],
                               in_=qT[0, o * K_PASS:(o + 1) * K_PASS, cols].rearrange("(p j) w -> p j w", j=PACK))
 
-        def load_words(o):
-            nc.sync.dma_start(out=pool_words[o][:].bitcast(I32), in_=k_words[o].rearrange("p t r -> p (t r)").bitcast(I32))
+        def load_words(o, first, end):
+            nc.sync.dma_start(out=pool_words[o][:, first:end].bitcast(I32),
+                              in_=k_words[o, :, first:end, :].rearrange("p t r -> p (t r)").bitcast(I32))
 
         nc.gpsimd.memset(pool_scales[:].bitcast(I32), 0)
         nc.gpsimd.memset(warm[:], 0.0)
         nc.scalar.copy(out=warm2[:], in_=warm[:])
         make_identity(nc, ident[:])
-        load_words(0)
+        load_words(0, 0, T)
         nc.sync.dma_start(offsets[:], offs)
         nc.sync.dma_start(out=ts_row[:], in_=ts[0].rearrange("(k m) -> k m", m=TS_PER_PART))
+        load_words(1, 0, T)
         load_q(0, slice(0, NQ))
-        load_words(1)
         for quad in range(4):
             nc.sync.dma_start(out=pool_scales[32 * quad:32 * quad + 4 * PASSES, :].bitcast(I32),
                               in_=k_scales[:, 4 * quad:4 * quad + 4, :].bitcast(I32))
         load_q(1, slice(0, NQ))
         load_q(2, block(0))
-        load_words(2)
+        load_words(2, 0, REACH)
         load_q(2, block(1))
+        load_words(2, REACH, T)
 
         rows = [keep.tile([P, T], F32, name=f"rows{b}") for b in range(BLOCKS)]
         for b in range(BLOCKS):
@@ -107,7 +109,7 @@ def tile_attend_sddmm_ts_srt_kernel(tc, qT, k_words, k_scales, ts, offs, out):
 
         def gather_words(o, s0, n):
             nc.vector.tensor_copy(out=key_words[o][:, s0:s0 + n],
-                                  in_=pool_words[o][:].indirect(offsets[:, s0 // 16:(s0 + n) // 16]))
+                                  in_=pool_words[o][:, :T - N + s0 + n].indirect(offsets[:, s0 // 16:(s0 + n) // 16]))
 
         last = PASSES - 1
         ts_listed = keep.tile([P, N], F32, name="ts_listed")

@@ -13,18 +13,30 @@ U32 = mybir.dt.uint32
 U16 = mybir.dt.uint16
 U8 = mybir.dt.uint8
 FP8X4 = mybir.dt.float8_e4m3fn_x4
-MULT = mybir.AluOpType.mult
 
 P = 128
 PACK = 4
 K_PASS = P * PACK
 PASSES = D // K_PASS
+LAST = PASSES - 1
+QUADRANT = 32
+SCALE_ROWS = 4
+PER_COLUMN = 16
 BLOCKS = NQ // P
-HALVES = 2
-HALF = N // HALVES
-LIST_COLS = N // 16
-TS_PER_PART = T // P
-REACH = T - N + HALF
+HALF = N // 2
+LINE = 4
+TS_PER_PARTITION = T // P
+PER_BANK = 4
+
+PARTS = [(0, 0, HALF), (0, HALF, HALF), (1, 0, N)]
+
+
+def block(b):
+    return slice(b * P, (b + 1) * P)
+
+
+def reach(end_slot):
+    return T - (N - end_slot)
 
 
 def tile_attend_sddmm_ts_srt_kernel(tc, qT, k_words, k_scales, ts, offs, out):
@@ -33,103 +45,128 @@ def tile_attend_sddmm_ts_srt_kernel(tc, qT, k_words, k_scales, ts, offs, out):
         keep = ctx.enter_context(tc.tile_pool(name="keep", bufs=1))
         psum = ctx.enter_context(tc.psum_pool(name="psum", bufs=1))
 
-        offsets = keep.tile([P, LIST_COLS], U16, name="offsets")
-        ts_row = keep.tile([P, TS_PER_PART], F32, name="ts_row")
+        offsets = keep.tile([P, N // PER_COLUMN], U16, name="offsets")
+        ts_row = keep.tile([P, TS_PER_PARTITION], F32, name="ts_row")
         q_raw = [keep.tile([P, PACK, NQ], F32, name=f"q_raw{o}") for o in range(PASSES)]
         pool_words = [keep.tile([P, T], U32, name=f"pool_words{o}") for o in range(PASSES)]
         pool_scales = keep.tile([P, T], U8, name="pool_scales", align_bytes=64)
         ident = keep.tile([P, P], F32, name="ident")
-        warm = keep.tile([P, 8], F32, name="warm")
-        warm2 = keep.tile([P, 8], F32, name="warm2")
 
-        def block(b):
-            return slice(b * P, (b + 1) * P)
-
-        def load_q(o, cols):
-            nc.sync.dma_start(out=q_raw[o][:, :, cols],
-                              in_=qT[0, o * K_PASS:(o + 1) * K_PASS, cols].rearrange("(p j) w -> p j w", j=PACK))
+        def load_q(o, queries):
+            nc.sync.dma_start(
+                out=q_raw[o][:, :, queries],
+                in_=qT[0, o * K_PASS:(o + 1) * K_PASS, queries].rearrange("(p j) w -> p j w", j=PACK),
+            )
 
         def load_words(o, first, end):
-            nc.sync.dma_start(out=pool_words[o][:, first:end].bitcast(I32),
-                              in_=k_words[o, :, first:end, :].rearrange("p t r -> p (t r)").bitcast(I32))
+            nc.sync.dma_start(
+                out=pool_words[o][:, first:end].bitcast(I32),
+                in_=k_words[o, :, first:end, :].rearrange("p t r -> p (t r)").bitcast(I32),
+            )
+
+        def entries(first_slot, slots):
+            return offsets[:, first_slot // PER_COLUMN:(first_slot + slots) // PER_COLUMN]
 
         nc.gpsimd.memset(pool_scales[:].bitcast(I32), 0)
-        nc.gpsimd.memset(warm[:], 0.0)
-        nc.scalar.copy(out=warm2[:], in_=warm[:])
         make_identity(nc, ident[:])
+
         load_words(0, 0, T)
         nc.sync.dma_start(offsets[:], offs)
-        nc.sync.dma_start(out=ts_row[:], in_=ts[0].rearrange("(k m) -> k m", m=TS_PER_PART))
+        nc.sync.dma_start(out=ts_row[:], in_=ts[0].rearrange("(k m) -> k m", m=TS_PER_PARTITION))
         load_words(1, 0, T)
         load_q(0, slice(0, NQ))
-        for quad in range(4):
-            nc.sync.dma_start(out=pool_scales[32 * quad:32 * quad + 4 * PASSES, :].bitcast(I32),
-                              in_=k_scales[:, 4 * quad:4 * quad + 4, :].bitcast(I32))
+        for quad in range(P // QUADRANT):
+            nc.sync.dma_start(
+                out=pool_scales[QUADRANT * quad:QUADRANT * quad + SCALE_ROWS * PASSES, :].bitcast(I32),
+                in_=k_scales[:, SCALE_ROWS * quad:SCALE_ROWS * (quad + 1), :].bitcast(I32),
+            )
         load_q(1, slice(0, NQ))
-        load_q(2, block(0))
-        load_words(2, 0, REACH)
-        load_q(2, block(1))
-        load_words(2, REACH, T)
+        load_q(LAST, block(0))
+        load_words(LAST, 0, reach(HALF))
+        load_q(LAST, block(1))
+        load_words(LAST, reach(HALF), T)
 
         rows = [keep.tile([P, T], F32, name=f"rows{b}") for b in range(BLOCKS)]
         for b in range(BLOCKS):
             nc.vector.memset(rows[b][:], 0.0)
 
         ts_pool = keep.tile([P, T], F32, name="ts_pool")
-        for g in range(2):
-            spread = psum.tile([P, 4, P], F32, name=f"spread{g}")
-            for m in range(4):
-                col = 4 * g + m
+        banks = TS_PER_PARTITION // PER_BANK
+        for g in range(banks):
+            spread = psum.tile([P, PER_BANK, P], F32, name=f"spread{g}")
+            for m in range(PER_BANK):
+                col = PER_BANK * g + m
                 nc.tensor.transpose(spread[:, m, :], ts_row[:, col:col + 1].to_broadcast([P, P]), ident[:])
-            nc.scalar.copy(out=ts_pool[:].rearrange("p (k g m) -> p k g m", g=2, m=4)[:, :, g, :],
-                           in_=spread[:].rearrange("p m k -> p k m"))
+            nc.scalar.copy(
+                out=ts_pool[:].rearrange("p (k g m) -> p k g m", g=banks, m=PER_BANK)[:, :, g, :],
+                in_=spread[:].rearrange("p m k -> p k m"),
+            )
 
         q_codes = [keep.tile([P, NQ], U32, name=f"q_codes{o}", align_bytes=64) for o in range(PASSES)]
         q_scales = [keep.tile([P, NQ], U8, name=f"q_scales{o}", align_bytes=64) for o in range(PASSES)]
 
-        def quantize(o, cols, tag):
-            width = cols.stop - cols.start
-            grouped = keep.tile([P, width, PACK], BF16, name="grouped", tag=tag, align_bytes=64)
-            nc.scalar.copy(out=grouped[:].rearrange("p (c i) j -> p c j i", i=4),
-                           in_=q_raw[o][:, :, cols].rearrange("p j (c i) -> p c j i", i=4))
-            nc.vector.quantize_mx(out=q_codes[o][:, cols].bitcast(FP8X4), scales=q_scales[o][:, cols],
-                                  in_=grouped[:].rearrange("p w j -> p (w j)"))
+        def quantize(o, queries):
+            width = queries.stop - queries.start
+            grouped = keep.tile([P, width, PACK], BF16, name=f"grouped{o}_{queries.start}", align_bytes=64)
+            nc.scalar.copy(
+                out=grouped[:].rearrange("p (c i) j -> p c j i", i=LINE),
+                in_=q_raw[o][:, :, queries].rearrange("p j (c i) -> p c j i", i=LINE),
+            )
+            nc.vector.quantize_mx(
+                out=q_codes[o][:, queries].bitcast(FP8X4),
+                scales=q_scales[o][:, queries],
+                in_=grouped[:].rearrange("p w j -> p (w j)"),
+            )
 
         key_words = [keep.tile([P, N], U32, name=f"key_words{o}", align_bytes=64) for o in range(PASSES)]
         key_scales = keep.tile([P, N], U8, name="key_scales", align_bytes=64)
-        parts = [(0, 0, HALF), (0, HALF, HALF), (1, 0, N)]
-        acc = [psum.tile([P, n], F32, name=f"acc{b}_{s0}") for b, s0, n in parts]
-        scores = [keep.tile([P, n], F32, name=f"scores{b}_{s0}") for b, s0, n in parts]
-
-        def multiply(o, i):
-            b, s0, n = parts[i]
-            nc.tensor.matmul_mx(out=acc[i][:], lhsT=q_codes[o][:, block(b)].bitcast(FP8X4), lhsT_scale=q_scales[o][:, block(b)],
-                                rhs=key_words[o][:, s0:s0 + n].bitcast(FP8X4), rhs_scale=key_scales[4 * o:P, s0:s0 + n],
-                                start=(o == 0), stop=(o == PASSES - 1))
-
-        def gather_words(o, s0, n):
-            nc.vector.tensor_copy(out=key_words[o][:, s0:s0 + n],
-                                  in_=pool_words[o][:, :T - N + s0 + n].indirect(offsets[:, s0 // 16:(s0 + n) // 16]))
-
-        last = PASSES - 1
+        acc = [psum.tile([P, slots], F32, name=f"acc{b}_{first}") for b, first, slots in PARTS]
+        scores = [keep.tile([P, slots], F32, name=f"scores{b}_{first}") for b, first, slots in PARTS]
         ts_listed = keep.tile([P, N], F32, name="ts_listed")
+
+        def multiply(o, part):
+            b, first, slots = PARTS[part]
+            nc.tensor.matmul_mx(
+                out=acc[part][:],
+                lhsT=q_codes[o][:, block(b)].bitcast(FP8X4),
+                lhsT_scale=q_scales[o][:, block(b)],
+                rhs=key_words[o][:, first:first + slots].bitcast(FP8X4),
+                rhs_scale=key_scales[SCALE_ROWS * o:P, first:first + slots],
+                start=(o == 0),
+                stop=(o == LAST),
+            )
+
+        def gather_words(o, first, slots):
+            nc.vector.tensor_copy(
+                out=key_words[o][:, first:first + slots],
+                in_=pool_words[o][:, :reach(first + slots)].indirect(entries(first, slots)),
+            )
+
+        def finish(part):
+            multiply(LAST, part)
+            nc.scalar.copy(out=scores[part][:], in_=acc[part][:])
+
         nc.vector.tensor_copy(out=key_scales[:], in_=pool_scales[:].indirect(offsets[:]))
-        for o in range(last):
+        for o in range(LAST):
             gather_words(o, 0, N)
-            quantize(o, slice(0, NQ), f"grouped{o}")
-            for i in range(len(parts)):
-                multiply(o, i)
-        quantize(last, block(0), "grouped_a")
+            quantize(o, slice(0, NQ))
+            for part in range(len(PARTS)):
+                multiply(o, part)
+        quantize(LAST, block(0))
         nc.vector.tensor_copy(out=ts_listed[:], in_=ts_pool[:].indirect(offsets[:]))
-        for i in range(2):
-            gather_words(last, i * HALF, HALF)
-            multiply(last, i)
-            nc.scalar.copy(out=scores[i][:], in_=acc[i][:])
-        quantize(last, block(1), "grouped_b")
-        multiply(last, 2)
-        nc.scalar.copy(out=scores[2][:], in_=acc[2][:])
-        for i, (b, s0, n) in enumerate(parts):
-            nc.vector.tensor_tensor(rows[b][:].indirect(offsets[:, s0 // 16:(s0 + n) // 16]), scores[i][:],
-                                    ts_listed[:, s0:s0 + n], MULT)
-            if s0 + n == N:
+        for part, (b, first, slots) in enumerate(PARTS):
+            if b == 0:
+                gather_words(LAST, first, slots)
+            else:
+                quantize(LAST, block(b))
+            finish(part)
+
+        for part, (b, first, slots) in enumerate(PARTS):
+            nc.vector.tensor_tensor(
+                rows[b][:].indirect(entries(first, slots)),
+                scores[part][:],
+                ts_listed[:, first:first + slots],
+                mybir.AluOpType.mult,
+            )
+            if first + slots == N:
                 nc.sync.dma_start(out=out[0, block(b), :], in_=rows[b][:])

@@ -28,7 +28,9 @@ LINE = 4
 TS_PER_PARTITION = T // P
 PER_BANK = 4
 
-PARTS = [(0, 0, HALF), (0, HALF, HALF), (1, 0, N)]
+PARTS = [(b, first) for b in range(BLOCKS) for first in (0, HALF)]
+WORDS_BYTES = 4 * N
+STAGED_BLOCK_BYTES = 2 * PACK * P
 
 
 def block(b):
@@ -43,18 +45,23 @@ def tile_attend_sddmm_ts_srt_kernel(tc, qT, k_words, k_scales, ts, offs, out):
     nc = tc.nc
     with ExitStack() as ctx:
         keep = ctx.enter_context(tc.tile_pool(name="keep", bufs=1))
+        placed = ctx.enter_context(tc.tile_pool(name="placed", bufs=1))
         psum = ctx.enter_context(tc.psum_pool(name="psum", bufs=1))
 
         offsets = keep.tile([P, N // PER_COLUMN], U16, name="offsets")
-        ts_row = keep.tile([P, TS_PER_PARTITION], F32, name="ts_row")
-        q_raw = [keep.tile([P, PACK, NQ], F32, name=f"q_raw{o}") for o in range(PASSES)]
-        pool_words = [keep.tile([P, T], U32, name=f"pool_words{o}") for o in range(PASSES)]
+        ts_row = keep.tile([P, TS_PER_PARTITION], F32, name="ts_row", tag="after_ts_row", align_bytes=64)
+        raw0 = keep.tile([P, PACK, NQ], F32, name="raw0", tag="after_raw0", align_bytes=64)
+        raw1 = placed.tile([P, PACK, NQ], F32, name="raw1", align_bytes=64, offset=0)
+        raw_last = [keep.tile([P, PACK, P], F32, name=f"raw_last{b}") for b in range(BLOCKS)]
+        pool_words = [
+            keep.tile([P, T], U32, name=f"pool_words{o}", tag=f"after_words{o}", align_bytes=64) for o in range(PASSES)
+        ]
         pool_scales = keep.tile([P, T], U8, name="pool_scales", align_bytes=64)
         ident = keep.tile([P, P], F32, name="ident")
 
-        def load_q(o, queries):
+        def load_q(raw, o, queries):
             nc.sync.dma_start(
-                out=q_raw[o][:, :, queries],
+                out=raw[:],
                 in_=qT[0, o * K_PASS:(o + 1) * K_PASS, queries].rearrange("(p j) w -> p j w", j=PACK),
             )
 
@@ -70,27 +77,27 @@ def tile_attend_sddmm_ts_srt_kernel(tc, qT, k_words, k_scales, ts, offs, out):
         nc.gpsimd.memset(pool_scales[:].bitcast(I32), 0)
         make_identity(nc, ident[:])
 
+        nc.sync.dma_start(out=ts_row[:], in_=ts[0].rearrange("(k m) -> k m", m=TS_PER_PARTITION))
         load_words(0, 0, T)
         nc.sync.dma_start(offsets[:], offs)
-        nc.sync.dma_start(out=ts_row[:], in_=ts[0].rearrange("(k m) -> k m", m=TS_PER_PARTITION))
-        load_words(1, 0, T)
-        load_q(0, slice(0, NQ))
+        load_q(raw0, 0, slice(0, NQ))
+        load_q(raw1, 1, slice(0, NQ))
         for quad in range(P // QUADRANT):
             nc.sync.dma_start(
                 out=pool_scales[QUADRANT * quad:QUADRANT * quad + SCALE_ROWS * PASSES, :].bitcast(I32),
                 in_=k_scales[:, SCALE_ROWS * quad:SCALE_ROWS * (quad + 1), :].bitcast(I32),
             )
-        load_q(1, slice(0, NQ))
-        load_q(LAST, block(0))
+        load_q(raw_last[0], LAST, block(0))
+        load_words(1, 0, T)
         load_words(LAST, 0, reach(HALF))
-        load_q(LAST, block(1))
+        load_q(raw_last[1], LAST, block(1))
         load_words(LAST, reach(HALF), T)
 
         rows = [keep.tile([P, T], F32, name=f"rows{b}") for b in range(BLOCKS)]
         for b in range(BLOCKS):
             nc.vector.memset(rows[b][:], 0.0)
 
-        ts_pool = keep.tile([P, T], F32, name="ts_pool")
+        ts_pool = keep.tile([P, T], F32, name="ts_pool", tag="after_ts_pool", align_bytes=64)
         banks = TS_PER_PARTITION // PER_BANK
         for g in range(banks):
             spread = psum.tile([P, PER_BANK, P], F32, name=f"spread{g}")
@@ -105,36 +112,23 @@ def tile_attend_sddmm_ts_srt_kernel(tc, qT, k_words, k_scales, ts, offs, out):
         q_codes = [keep.tile([P, NQ], U32, name=f"q_codes{o}", align_bytes=64) for o in range(PASSES)]
         q_scales = [keep.tile([P, NQ], U8, name=f"q_scales{o}", align_bytes=64) for o in range(PASSES)]
 
-        def quantize(o, queries):
-            width = queries.stop - queries.start
-            grouped = keep.tile([P, width, PACK], BF16, name=f"grouped{o}_{queries.start}", align_bytes=64)
-            nc.scalar.copy(
-                out=grouped[:].rearrange("p (c i) j -> p c j i", i=LINE),
-                in_=q_raw[o][:, :, queries].rearrange("p j (c i) -> p c j i", i=LINE),
+        def stage(copy, staged, raw):
+            copy(
+                out=staged[:].rearrange("p (c i) j -> p c j i", i=LINE),
+                in_=raw[:].rearrange("p j (c i) -> p c j i", i=LINE),
             )
+
+        def quantize(o, queries, staged):
             nc.vector.quantize_mx(
                 out=q_codes[o][:, queries].bitcast(FP8X4),
                 scales=q_scales[o][:, queries],
-                in_=grouped[:].rearrange("p w j -> p (w j)"),
+                in_=staged[:].rearrange("p w j -> p (w j)"),
             )
 
-        key_words = [keep.tile([P, N], U32, name=f"key_words{o}", align_bytes=64) for o in range(PASSES)]
-        key_scales = keep.tile([P, N], U8, name="key_scales", align_bytes=64)
-        acc = [psum.tile([P, slots], F32, name=f"acc{b}_{first}") for b, first, slots in PARTS]
-        scores = [keep.tile([P, slots], F32, name=f"scores{b}_{first}") for b, first, slots in PARTS]
+        acc = [psum.tile([P, HALF], F32, name=f"acc{b}_{first}") for b, first in PARTS]
+        scores = [keep.tile([P, N], F32, name=f"scores{b}") for b in range(BLOCKS)]
         ts_listed = keep.tile([P, N], F32, name="ts_listed")
-
-        def multiply(o, part):
-            b, first, slots = PARTS[part]
-            nc.tensor.matmul_mx(
-                out=acc[part][:],
-                lhsT=q_codes[o][:, block(b)].bitcast(FP8X4),
-                lhsT_scale=q_scales[o][:, block(b)],
-                rhs=key_words[o][:, first:first + slots].bitcast(FP8X4),
-                rhs_scale=key_scales[SCALE_ROWS * o:P, first:first + slots],
-                start=(o == 0),
-                stop=(o == LAST),
-            )
+        key_words = [keep.tile([P, N], U32, name="key_words0", align_bytes=64)]
 
         def gather_words(o, first, slots):
             nc.vector.tensor_copy(
@@ -142,29 +136,65 @@ def tile_attend_sddmm_ts_srt_kernel(tc, qT, k_words, k_scales, ts, offs, out):
                 in_=pool_words[o][:, :reach(first + slots)].indirect(entries(first, slots)),
             )
 
-        def finish(part):
-            multiply(LAST, part)
-            nc.scalar.copy(out=scores[part][:], in_=acc[part][:])
-
-        nc.vector.tensor_copy(out=key_scales[:], in_=pool_scales[:].indirect(offsets[:]))
-        for o in range(LAST):
-            gather_words(o, 0, N)
-            quantize(o, slice(0, NQ))
-            for part in range(len(PARTS)):
-                multiply(o, part)
-        quantize(LAST, block(0))
+        gather_words(0, 0, N)
         nc.vector.tensor_copy(out=ts_listed[:], in_=ts_pool[:].indirect(offsets[:]))
-        for part, (b, first, slots) in enumerate(PARTS):
-            if b == 0:
-                gather_words(LAST, first, slots)
-            else:
-                quantize(LAST, block(b))
-            finish(part)
 
-        for part, (b, first, slots) in enumerate(PARTS):
+        staged0 = keep.tile([P, NQ, PACK], BF16, name="staged0", tag="after_ts_row", align_bytes=64)
+        stage(nc.scalar.copy, staged0, raw0)
+        quantize(0, slice(0, NQ), staged0)
+        key_scales = keep.tile([P, N], U8, name="key_scales", tag="after_ts_pool", align_bytes=64)
+        nc.vector.tensor_copy(out=key_scales[:], in_=pool_scales[:].indirect(offsets[:]))
+
+        def multiply(o, part):
+            b, first = PARTS[part]
+            nc.tensor.matmul_mx(
+                out=acc[part][:],
+                lhsT=q_codes[o][:, block(b)].bitcast(FP8X4),
+                lhsT_scale=q_scales[o][:, block(b)],
+                rhs=key_words[o][:, first:first + HALF].bitcast(FP8X4),
+                rhs_scale=key_scales[SCALE_ROWS * o:P, first:first + HALF],
+                start=(o == 0),
+                stop=(o == LAST),
+            )
+
+        for part in range(len(PARTS)):
+            multiply(0, part)
+
+        staged1 = keep.tile([P, NQ, PACK], BF16, name="staged1", tag="after_raw0", align_bytes=64)
+        stage(nc.scalar.copy, staged1, raw1)
+        quantize(1, slice(0, NQ), staged1)
+        staged_a = placed.tile([P, P, PACK], BF16, name="staged_a", align_bytes=64,
+                               offset=WORDS_BYTES - STAGED_BLOCK_BYTES // 2)
+        stage(nc.scalar.copy, staged_a, raw_last[0])
+        quantize(LAST, block(0), staged_a)
+        for o in (1, LAST):
+            key_words.append(placed.tile([P, N], U32, name=f"key_words{o}", align_bytes=64, offset=(o - 1) * WORDS_BYTES))
+
+        def finish(part):
+            b, first = PARTS[part]
+            multiply(LAST, part)
+            nc.scalar.copy(out=scores[b][:, first:first + HALF], in_=acc[part][:])
+
+        gather_words(1, 0, HALF)
+        multiply(1, 0)
+        gather_words(1, HALF, HALF)
+        multiply(1, 1)
+        gather_words(LAST, 0, HALF)
+        finish(0)
+        multiply(1, 2)
+        multiply(1, 3)
+        staged_b = keep.tile([P, P, PACK], BF16, name="staged_b", tag="after_words1", align_bytes=64)
+        stage(nc.vector.tensor_copy, staged_b, raw_last[1])
+        gather_words(LAST, HALF, HALF)
+        finish(1)
+        quantize(LAST, block(1), staged_b)
+        finish(2)
+        finish(3)
+
+        for b, first, slots in ((0, 0, HALF), (0, HALF, HALF), (1, 0, N)):
             nc.vector.tensor_tensor(
                 rows[b][:].indirect(entries(first, slots)),
-                scores[part][:],
+                scores[b][:, first:first + slots],
                 ts_listed[:, first:first + slots],
                 mybir.AluOpType.mult,
             )

@@ -52,10 +52,11 @@ def tile_attend_sddmm_ts_srt_kernel(tc, qT, k_words, k_scales, ts, offs, out):
         ts_row = keep.tile([P, TS_PER_PARTITION], F32, name="ts_row", tag="after_ts_row", align_bytes=64)
         raw0 = keep.tile([P, PACK, NQ], F32, name="raw0", tag="after_raw0", align_bytes=64)
         raw1 = placed.tile([P, PACK, NQ], F32, name="raw1", align_bytes=64, offset=0)
-        raw_last = [keep.tile([P, PACK, P], F32, name=f"raw_last{b}") for b in range(BLOCKS)]
-        pool_words = [
-            keep.tile([P, T], U32, name=f"pool_words{o}", tag=f"after_words{o}", align_bytes=64) for o in range(PASSES)
+        raw_last = [
+            keep.tile([P, PACK, P], F32, name=f"raw_last{b}", tag=f"after_raw_last{b}", align_bytes=64)
+            for b in range(BLOCKS)
         ]
+        pool_words = [keep.tile([P, T], U32, name=f"pool_words{o}") for o in range(PASSES)]
         pool_scales = keep.tile([P, T], U8, name="pool_scales", align_bytes=64)
         ident = keep.tile([P, P], F32, name="ident")
 
@@ -97,7 +98,7 @@ def tile_attend_sddmm_ts_srt_kernel(tc, qT, k_words, k_scales, ts, offs, out):
         for b in range(BLOCKS):
             nc.vector.memset(rows[b][:], 0.0)
 
-        ts_pool = keep.tile([P, T], F32, name="ts_pool", tag="after_ts_pool", align_bytes=64)
+        ts_pool = keep.tile([P, T], F32, name="ts_pool")
         banks = TS_PER_PARTITION // PER_BANK
         for g in range(banks):
             spread = psum.tile([P, PER_BANK, P], F32, name=f"spread{g}")
@@ -128,21 +129,22 @@ def tile_attend_sddmm_ts_srt_kernel(tc, qT, k_words, k_scales, ts, offs, out):
         acc = [psum.tile([P, HALF], F32, name=f"acc{b}_{first}") for b, first in PARTS]
         scores = [keep.tile([P, N], F32, name=f"scores{b}") for b in range(BLOCKS)]
         ts_listed = keep.tile([P, N], F32, name="ts_listed")
-        key_words = [keep.tile([P, N], U32, name="key_words0", align_bytes=64)]
+        words0 = keep.tile([P, N], U32, name="words0", align_bytes=64)
+        key_words = {(0, first): words0[:, first:first + HALF] for first in (0, HALF)}
 
-        def gather_words(o, first, slots):
+        def gather_words(o, first):
             nc.vector.tensor_copy(
-                out=key_words[o][:, first:first + slots],
-                in_=pool_words[o][:, :reach(first + slots)].indirect(entries(first, slots)),
+                out=key_words[o, first],
+                in_=pool_words[o][:, :reach(first + HALF)].indirect(entries(first, HALF)),
             )
 
-        gather_words(0, 0, N)
+        nc.vector.tensor_copy(out=words0[:], in_=pool_words[0][:].indirect(offsets[:]))
         nc.vector.tensor_copy(out=ts_listed[:], in_=ts_pool[:].indirect(offsets[:]))
 
         staged0 = keep.tile([P, NQ, PACK], BF16, name="staged0", tag="after_ts_row", align_bytes=64)
         stage(nc.scalar.copy, staged0, raw0)
         quantize(0, slice(0, NQ), staged0)
-        key_scales = keep.tile([P, N], U8, name="key_scales", tag="after_ts_pool", align_bytes=64)
+        key_scales = keep.tile([P, N], U8, name="key_scales", tag="after_ts_row", align_bytes=64)
         nc.vector.tensor_copy(out=key_scales[:], in_=pool_scales[:].indirect(offsets[:]))
 
         def multiply(o, part):
@@ -151,7 +153,7 @@ def tile_attend_sddmm_ts_srt_kernel(tc, qT, k_words, k_scales, ts, offs, out):
                 out=acc[part][:],
                 lhsT=q_codes[o][:, block(b)].bitcast(FP8X4),
                 lhsT_scale=q_scales[o][:, block(b)],
-                rhs=key_words[o][:, first:first + HALF].bitcast(FP8X4),
+                rhs=key_words[o, first].bitcast(FP8X4),
                 rhs_scale=key_scales[SCALE_ROWS * o:P, first:first + HALF],
                 start=(o == 0),
                 stop=(o == LAST),
@@ -166,26 +168,31 @@ def tile_attend_sddmm_ts_srt_kernel(tc, qT, k_words, k_scales, ts, offs, out):
         staged_a = placed.tile([P, P, PACK], BF16, name="staged_a", align_bytes=64,
                                offset=WORDS_BYTES - STAGED_BLOCK_BYTES // 2)
         stage(nc.scalar.copy, staged_a, raw_last[0])
-        quantize(LAST, block(0), staged_a)
-        for o in (1, LAST):
-            key_words.append(placed.tile([P, N], U32, name=f"key_words{o}", align_bytes=64, offset=(o - 1) * WORDS_BYTES))
 
         def finish(part):
             b, first = PARTS[part]
             multiply(LAST, part)
             nc.scalar.copy(out=scores[b][:, first:first + HALF], in_=acc[part][:])
 
-        gather_words(1, 0, HALF)
+        words1_low = keep.tile([P, HALF], U32, name="words1_low", tag="after_raw0", align_bytes=64)
+        key_words[1, 0] = words1_low[:]
+        gather_words(1, 0)
         multiply(1, 0)
-        gather_words(1, HALF, HALF)
+        quantize(LAST, block(0), staged_a)
+        words1_high = keep.tile([P, HALF], U32, name="words1_high", tag="after_raw_last0", align_bytes=64)
+        key_words[1, HALF] = words1_high[:]
+        gather_words(1, HALF)
         multiply(1, 1)
-        gather_words(LAST, 0, HALF)
+        words2 = placed.tile([P, N], U32, name="words2", align_bytes=64, offset=0)
+        for first in (0, HALF):
+            key_words[LAST, first] = words2[:, first:first + HALF]
+        gather_words(LAST, 0)
         finish(0)
         multiply(1, 2)
         multiply(1, 3)
-        staged_b = keep.tile([P, P, PACK], BF16, name="staged_b", tag="after_words1", align_bytes=64)
+        staged_b = placed.tile([P, P, PACK], BF16, name="staged_b", align_bytes=64, offset=WORDS_BYTES)
         stage(nc.vector.tensor_copy, staged_b, raw_last[1])
-        gather_words(LAST, HALF, HALF)
+        gather_words(LAST, HALF)
         finish(1)
         quantize(LAST, block(1), staged_b)
         finish(2)

@@ -29,6 +29,7 @@ TS_PER_PARTITION = T // P
 PER_BANK = 4
 
 PARTS = [(b, first) for b in range(BLOCKS) for first in (0, HALF)]
+LEAD = 128
 WORDS_BYTES = 4 * N
 STAGED_BLOCK_BYTES = 2 * PACK * P
 
@@ -91,8 +92,8 @@ def tile_attend_sddmm_ts_srt_kernel(tc, qT, k_words, k_scales, ts, offs, out):
         load_q(raw_last[0], LAST, block(0))
         load_words(1, 0, T)
         load_words(LAST, 0, reach(HALF))
-        load_q(raw_last[1], LAST, block(1))
         load_words(LAST, reach(HALF), T)
+        load_q(raw_last[1], LAST, block(1))
 
         rows = [keep.tile([P, T], F32, name=f"rows{b}") for b in range(BLOCKS)]
         for b in range(BLOCKS):
@@ -172,7 +173,8 @@ def tile_attend_sddmm_ts_srt_kernel(tc, qT, k_words, k_scales, ts, offs, out):
         def finish(part):
             b, first = PARTS[part]
             multiply(LAST, part)
-            nc.scalar.copy(out=scores[b][:, first:first + HALF], in_=acc[part][:])
+            for a, e in ((0, LEAD), (LEAD, HALF)) if part == 0 else ((0, HALF),):
+                nc.scalar.copy(out=scores[b][:, first + a:first + e], in_=acc[part][:, a:e])
 
         words1_low = keep.tile([P, HALF], U32, name="words1_low", tag="after_raw0", align_bytes=64)
         key_words[1, 0] = words1_low[:]
@@ -191,14 +193,14 @@ def tile_attend_sddmm_ts_srt_kernel(tc, qT, k_words, k_scales, ts, offs, out):
         multiply(1, 2)
         multiply(1, 3)
         staged_b = placed.tile([P, P, PACK], BF16, name="staged_b", align_bytes=64, offset=WORDS_BYTES)
-        stage(nc.vector.tensor_copy, staged_b, raw_last[1])
         gather_words(LAST, HALF)
         finish(1)
+        stage(nc.vector.tensor_copy, staged_b, raw_last[1])
         quantize(LAST, block(1), staged_b)
         finish(2)
         finish(3)
 
-        for b, first, slots in ((0, 0, HALF), (0, HALF, HALF), (1, 0, N)):
+        for b, first, slots in ((0, 0, LEAD), (0, LEAD, N - LEAD), (1, 0, N)):
             nc.vector.tensor_tensor(
                 rows[b][:].indirect(entries(first, slots)),
                 scores[b][:, first:first + slots],

@@ -28,10 +28,9 @@ LINE = 4
 TS_PER_PARTITION = T // P
 PER_BANK = 4
 
-PARTS = [(b, first) for b in range(BLOCKS) for first in (0, HALF)]
-LEAD = 128
-WORDS_BYTES = 4 * N
-STAGED_BLOCK_BYTES = 2 * PACK * P
+RAW_BYTES = 4 * PACK * P
+HALF_BYTES = 4 * HALF
+VECTOR_SHARE = 80
 
 
 def block(b):
@@ -49,17 +48,19 @@ def tile_attend_sddmm_ts_srt_kernel(tc, qT, k_words, k_scales, ts, offs, out):
         placed = ctx.enter_context(tc.tile_pool(name="placed", bufs=1))
         psum = ctx.enter_context(tc.psum_pool(name="psum", bufs=1))
 
+        def place(shape, dtype, name, offset):
+            return placed.tile(shape, dtype, name=name, align_bytes=64, offset=offset)
+
+        at_raw0, at_raw1, at_raw_a, at_raw_b = (n * RAW_BYTES for n in (0, 2, 4, 5))
         offsets = keep.tile([P, N // PER_COLUMN], U16, name="offsets")
         ts_row = keep.tile([P, TS_PER_PARTITION], F32, name="ts_row", tag="after_ts_row", align_bytes=64)
-        raw0 = keep.tile([P, PACK, NQ], F32, name="raw0", tag="after_raw0", align_bytes=64)
-        raw1 = placed.tile([P, PACK, NQ], F32, name="raw1", align_bytes=64, offset=0)
-        raw_last = [
-            keep.tile([P, PACK, P], F32, name=f"raw_last{b}", tag=f"after_raw_last{b}", align_bytes=64)
-            for b in range(BLOCKS)
-        ]
+        raw0 = place([P, PACK, NQ], F32, "raw0", at_raw0)
+        raw1 = place([P, PACK, NQ], F32, "raw1", at_raw1)
+        raw_a = place([P, PACK, P], F32, "raw_a", at_raw_a)
+        raw_b = place([P, PACK, P], F32, "raw_b", at_raw_b)
         pool_words = [keep.tile([P, T], U32, name=f"pool_words{o}") for o in range(PASSES)]
         pool_scales = keep.tile([P, T], U8, name="pool_scales", align_bytes=64)
-        ident = keep.tile([P, P], F32, name="ident")
+        ident = keep.tile([P, P], F32, name="ident", tag="after_ident", align_bytes=64)
 
         def load_q(raw, o, queries):
             nc.sync.dma_start(
@@ -89,11 +90,12 @@ def tile_attend_sddmm_ts_srt_kernel(tc, qT, k_words, k_scales, ts, offs, out):
                 out=pool_scales[QUADRANT * quad:QUADRANT * quad + SCALE_ROWS * PASSES, :].bitcast(I32),
                 in_=k_scales[:, SCALE_ROWS * quad:SCALE_ROWS * (quad + 1), :].bitcast(I32),
             )
-        load_q(raw_last[0], LAST, block(0))
-        load_words(1, 0, T)
+        load_q(raw_a, LAST, block(0))
+        load_words(1, 0, reach(HALF))
         load_words(LAST, 0, reach(HALF))
+        load_q(raw_b, LAST, block(1))
+        load_words(1, reach(HALF), T)
         load_words(LAST, reach(HALF), T)
-        load_q(raw_last[1], LAST, block(1))
 
         rows = [keep.tile([P, T], F32, name=f"rows{b}") for b in range(BLOCKS)]
         for b in range(BLOCKS):
@@ -114,10 +116,10 @@ def tile_attend_sddmm_ts_srt_kernel(tc, qT, k_words, k_scales, ts, offs, out):
         q_codes = [keep.tile([P, NQ], U32, name=f"q_codes{o}", align_bytes=64) for o in range(PASSES)]
         q_scales = [keep.tile([P, NQ], U8, name=f"q_scales{o}", align_bytes=64) for o in range(PASSES)]
 
-        def stage(copy, staged, raw):
+        def stage(copy, staged, raw, queries):
             copy(
-                out=staged[:].rearrange("p (c i) j -> p c j i", i=LINE),
-                in_=raw[:].rearrange("p j (c i) -> p c j i", i=LINE),
+                out=staged[:, queries, :].rearrange("p (c i) j -> p c j i", i=LINE),
+                in_=raw[:, :, queries].rearrange("p j (c i) -> p c j i", i=LINE),
             )
 
         def quantize(o, queries, staged):
@@ -127,85 +129,86 @@ def tile_attend_sddmm_ts_srt_kernel(tc, qT, k_words, k_scales, ts, offs, out):
                 in_=staged[:].rearrange("p w j -> p (w j)"),
             )
 
-        acc = [psum.tile([P, HALF], F32, name=f"acc{b}_{first}") for b, first in PARTS]
+        acc = {(b, first): psum.tile([P, HALF], F32, name=f"acc{b}_{first}")
+               for first in (0, HALF) for b in range(BLOCKS)}
         scores = [keep.tile([P, N], F32, name=f"scores{b}") for b in range(BLOCKS)]
         ts_listed = keep.tile([P, N], F32, name="ts_listed")
         words0 = keep.tile([P, N], U32, name="words0", align_bytes=64)
         key_words = {(0, first): words0[:, first:first + HALF] for first in (0, HALF)}
 
-        def gather_words(o, first):
+        def gather_words(o, first, offset):
+            key_words[o, first] = place([P, HALF], U32, f"words{o}_{first}", offset)[:]
             nc.vector.tensor_copy(
                 out=key_words[o, first],
                 in_=pool_words[o][:, :reach(first + HALF)].indirect(entries(first, HALF)),
+            )
+
+        def multiply(o, b, first, stop=False):
+            nc.tensor.matmul_mx(
+                out=acc[b, first][:],
+                lhsT=q_codes[o][:, block(b)].bitcast(FP8X4),
+                lhsT_scale=q_scales[o][:, block(b)],
+                rhs=key_words[o, first].bitcast(FP8X4),
+                rhs_scale=key_scales[SCALE_ROWS * o:P, first:first + HALF],
+                start=(o == 0),
+                stop=stop,
             )
 
         nc.vector.tensor_copy(out=words0[:], in_=pool_words[0][:].indirect(offsets[:]))
         nc.vector.tensor_copy(out=ts_listed[:], in_=ts_pool[:].indirect(offsets[:]))
 
         staged0 = keep.tile([P, NQ, PACK], BF16, name="staged0", tag="after_ts_row", align_bytes=64)
-        stage(nc.scalar.copy, staged0, raw0)
+        stage(nc.scalar.copy, staged0, raw0, slice(0, NQ))
         quantize(0, slice(0, NQ), staged0)
-        key_scales = keep.tile([P, N], U8, name="key_scales", tag="after_ts_row", align_bytes=64)
+        key_scales = place([P, N], U8, "key_scales", at_raw0)
         nc.vector.tensor_copy(out=key_scales[:], in_=pool_scales[:].indirect(offsets[:]))
+        for b, first in acc:
+            multiply(0, b, first)
 
-        def multiply(o, part):
-            b, first = PARTS[part]
-            nc.tensor.matmul_mx(
-                out=acc[part][:],
-                lhsT=q_codes[o][:, block(b)].bitcast(FP8X4),
-                lhsT_scale=q_scales[o][:, block(b)],
-                rhs=key_words[o, first].bitcast(FP8X4),
-                rhs_scale=key_scales[SCALE_ROWS * o:P, first:first + HALF],
-                start=(o == 0),
-                stop=(o == LAST),
-            )
-
-        for part in range(len(PARTS)):
-            multiply(0, part)
-
-        staged1 = keep.tile([P, NQ, PACK], BF16, name="staged1", tag="after_raw0", align_bytes=64)
-        stage(nc.scalar.copy, staged1, raw1)
+        staged1 = keep.tile([P, NQ, PACK], BF16, name="staged1", tag="after_ident", align_bytes=64)
+        stage(nc.scalar.copy, staged1, raw1, slice(0, NQ))
         quantize(1, slice(0, NQ), staged1)
-        staged_a = placed.tile([P, P, PACK], BF16, name="staged_a", align_bytes=64,
-                               offset=WORDS_BYTES - STAGED_BLOCK_BYTES // 2)
-        stage(nc.scalar.copy, staged_a, raw_last[0])
+        gather_words(1, 0, at_raw1)
+        for b in range(BLOCKS):
+            multiply(1, b, 0)
 
-        def finish(part):
-            b, first = PARTS[part]
-            multiply(LAST, part)
-            for a, e in ((0, LEAD), (LEAD, HALF)) if part == 0 else ((0, HALF),):
-                nc.scalar.copy(out=scores[b][:, first + a:first + e], in_=acc[part][:, a:e])
-
-        words1_low = keep.tile([P, HALF], U32, name="words1_low", tag="after_raw0", align_bytes=64)
-        key_words[1, 0] = words1_low[:]
-        gather_words(1, 0)
-        multiply(1, 0)
+        at_staged_a = at_raw0 + HALF_BYTES
+        staged_a = place([P, P, PACK], BF16, "staged_a", at_staged_a)
+        stage(nc.scalar.copy, staged_a, raw_a, slice(0, P))
         quantize(LAST, block(0), staged_a)
-        words1_high = keep.tile([P, HALF], U32, name="words1_high", tag="after_raw_last0", align_bytes=64)
-        key_words[1, HALF] = words1_high[:]
-        gather_words(1, HALF)
-        multiply(1, 1)
-        words2 = placed.tile([P, N], U32, name="words2", align_bytes=64, offset=0)
-        for first in (0, HALF):
-            key_words[LAST, first] = words2[:, first:first + HALF]
-        gather_words(LAST, 0)
-        finish(0)
-        multiply(1, 2)
-        multiply(1, 3)
-        staged_b = placed.tile([P, P, PACK], BF16, name="staged_b", align_bytes=64, offset=WORDS_BYTES)
-        gather_words(LAST, HALF)
-        finish(1)
-        stage(nc.vector.tensor_copy, staged_b, raw_last[1])
-        quantize(LAST, block(1), staged_b)
-        finish(2)
-        finish(3)
+        gather_words(LAST, 0, at_raw_a)
+        multiply(LAST, 0, 0, stop=True)
 
-        for b, first, slots in ((0, 0, LEAD), (0, LEAD, N - LEAD), (1, 0, N)):
+        staged_b = place([P, P, PACK], BF16, "staged_b", at_raw_a + HALF_BYTES)
+        stage(nc.vector.tensor_copy, staged_b, raw_b, slice(0, VECTOR_SHARE))
+        stage(nc.scalar.copy, staged_b, raw_b, slice(VECTOR_SHARE, P))
+        gather_words(1, HALF, at_staged_a)
+        quantize(LAST, block(1), staged_b)
+        multiply(LAST, 1, 0, stop=True)
+        gather_words(LAST, HALF, at_raw_b)
+        for b in range(BLOCKS):
+            multiply(LAST, b, HALF)
+            multiply(1, b, HALF, stop=True)
+
+        def empty(b, first):
+            nc.scalar.copy(out=scores[b][:, first:first + HALF], in_=acc[b, first][:])
+
+        def scatter(b, first):
             nc.vector.tensor_tensor(
-                rows[b][:].indirect(entries(first, slots)),
-                scores[b][:, first:first + slots],
-                ts_listed[:, first:first + slots],
+                rows[b][:].indirect(entries(first, HALF)),
+                scores[b][:, first:first + HALF],
+                ts_listed[:, first:first + HALF],
                 mybir.AluOpType.mult,
             )
-            if first + slots == N:
-                nc.sync.dma_start(out=out[0, block(b), :], in_=rows[b][:])
+
+        for b in range(BLOCKS):
+            empty(b, 0)
+        for b, queue in enumerate((nc.sync, nc.scalar)):
+            scatter(b, 0)
+            empty(b, HALF)
+            early = keep.tile([P, HALF], F32, name=f"early{b}")
+            nc.scalar.copy(out=early[:], in_=rows[b][:, :HALF])
+            queue.dma_start(out=out[0, block(b), :HALF], in_=early[:])
+        for b in range(BLOCKS):
+            scatter(b, HALF)
+            nc.sync.dma_start(out=out[0, block(b), HALF:], in_=rows[b][:, HALF:])

@@ -91,11 +91,10 @@ def tile_attend_sddmm_ts_srt_kernel(tc, qT, k_words, k_scales, ts, offs, out):
                 in_=k_scales[:, SCALE_ROWS * quad:SCALE_ROWS * (quad + 1), :].bitcast(I32),
             )
         load_q(raw_a, LAST, block(0))
-        load_words(1, 0, reach(HALF))
+        load_words(1, 0, T)
         load_words(LAST, 0, reach(HALF))
-        load_q(raw_b, LAST, block(1))
-        load_words(1, reach(HALF), T)
         load_words(LAST, reach(HALF), T)
+        load_q(raw_b, LAST, block(1))
 
         rows = [keep.tile([P, T], F32, name=f"rows{b}") for b in range(BLOCKS)]
         for b in range(BLOCKS):
@@ -168,47 +167,28 @@ def tile_attend_sddmm_ts_srt_kernel(tc, qT, k_words, k_scales, ts, offs, out):
         staged1 = keep.tile([P, NQ, PACK], BF16, name="staged1", tag="after_ident", align_bytes=64)
         stage(nc.scalar.copy, staged1, raw1, slice(0, NQ))
         quantize(1, slice(0, NQ), staged1)
-        gather_words(1, 0, at_raw1)
-        for b in range(BLOCKS):
-            multiply(1, b, 0)
+        for first in (0, HALF):
+            gather_words(1, first, at_raw1 + 4 * first)
+            for b in range(BLOCKS):
+                multiply(1, b, first)
 
-        at_staged_a = at_raw0 + HALF_BYTES
-        staged_a = place([P, P, PACK], BF16, "staged_a", at_staged_a)
+        at_staged = at_raw0 + HALF_BYTES
+        staged_a = place([P, P, PACK], BF16, "staged_a", at_staged)
         stage(nc.scalar.copy, staged_a, raw_a, slice(0, P))
         quantize(LAST, block(0), staged_a)
-        gather_words(LAST, 0, at_raw_a)
-        multiply(LAST, 0, 0, stop=True)
+        for first in (0, HALF):
+            gather_words(LAST, first, at_raw_a + 4 * first)
+            multiply(LAST, 0, first, stop=True)
 
-        staged_b = place([P, P, PACK], BF16, "staged_b", at_raw_a + HALF_BYTES)
+        staged_b = place([P, P, PACK], BF16, "staged_b", at_staged)
         stage(nc.vector.tensor_copy, staged_b, raw_b, slice(0, VECTOR_SHARE))
         stage(nc.scalar.copy, staged_b, raw_b, slice(VECTOR_SHARE, P))
-        gather_words(1, HALF, at_staged_a)
         quantize(LAST, block(1), staged_b)
-        multiply(LAST, 1, 0, stop=True)
-        gather_words(LAST, HALF, at_raw_b)
-        for b in range(BLOCKS):
-            multiply(LAST, b, HALF)
-            multiply(1, b, HALF, stop=True)
-
-        def empty(b, first):
-            nc.scalar.copy(out=scores[b][:, first:first + HALF], in_=acc[b, first][:])
-
-        def scatter(b, first):
-            nc.vector.tensor_tensor(
-                rows[b][:].indirect(entries(first, HALF)),
-                scores[b][:, first:first + HALF],
-                ts_listed[:, first:first + HALF],
-                mybir.AluOpType.mult,
-            )
+        for first in (0, HALF):
+            multiply(LAST, 1, first, stop=True)
 
         for b in range(BLOCKS):
-            empty(b, 0)
-        for b, queue in enumerate((nc.sync, nc.scalar)):
-            scatter(b, 0)
-            empty(b, HALF)
-            early = keep.tile([P, HALF], F32, name=f"early{b}")
-            nc.scalar.copy(out=early[:], in_=rows[b][:, :HALF])
-            queue.dma_start(out=out[0, block(b), :HALF], in_=early[:])
-        for b in range(BLOCKS):
-            scatter(b, HALF)
-            nc.sync.dma_start(out=out[0, block(b), HALF:], in_=rows[b][:, HALF:])
+            for first in (0, HALF):
+                nc.scalar.copy(out=scores[b][:, first:first + HALF], in_=acc[b, first][:])
+            nc.vector.tensor_tensor(rows[b][:].indirect(offsets[:]), scores[b][:], ts_listed[:], mybir.AluOpType.mult)
+            nc.sync.dma_start(out=out[0, block(b), :], in_=rows[b][:])

@@ -77,8 +77,9 @@ def tile_attend_sddmm_ts_srt_kernel(tc, qT, k_words, k_scales, ts, offs, out):
         def entries(first_slot, slots):
             return offsets[:, first_slot // PER_COLUMN:(first_slot + slots) // PER_COLUMN]
 
-        nc.gpsimd.memset(pool_scales[:].bitcast(I32), 0)
-        make_identity(nc, ident[:])
+        nc.vector.memset(ident[:], 0.0)
+        nc.vector.memset(pool_scales[:].bitcast(I32), 0)
+        make_identity(nc, ident[:], nomemset=True)
 
         nc.sync.dma_start(out=ts_row[:], in_=ts[0].rearrange("(k m) -> k m", m=TS_PER_PARTITION))
         load_words(0, 0, T)
@@ -86,7 +87,7 @@ def tile_attend_sddmm_ts_srt_kernel(tc, qT, k_words, k_scales, ts, offs, out):
         load_q(raw0, 0, slice(0, NQ))
         load_q(raw1, 1, slice(0, NQ))
         for quad in range(P // QUADRANT):
-            nc.sync.dma_start(
+            (nc.gpsimd if quad == 0 else nc.sync).dma_start(
                 out=pool_scales[QUADRANT * quad:QUADRANT * quad + SCALE_ROWS * PASSES, :].bitcast(I32),
                 in_=k_scales[:, SCALE_ROWS * quad:SCALE_ROWS * (quad + 1), :].bitcast(I32),
             )

@@ -28,9 +28,11 @@ LINE = 4
 TS_PER_PARTITION = T // P
 PER_BANK = 4
 
-RAW_BYTES = 4 * PACK * P
-HALF_BYTES = 4 * HALF
-VECTOR_SHARE = 80
+COPY = mybir.ActivationFunctionType.Copy
+MULT = mybir.AluOpType.mult
+RAW_BYTES = 4 * PACK * NQ
+WORDS_BYTES = 4 * N
+VECTOR_SHARE = 168
 
 
 def block(b):
@@ -51,21 +53,17 @@ def tile_attend_sddmm_ts_srt_kernel(tc, qT, k_words, k_scales, ts, offs, out):
         def place(shape, dtype, name, offset):
             return placed.tile(shape, dtype, name=name, align_bytes=64, offset=offset)
 
-        at_raw0, at_raw1, at_raw_a, at_raw_b = (n * RAW_BYTES for n in (0, 2, 4, 5))
         offsets = keep.tile([P, N // PER_COLUMN], U16, name="offsets")
         ts_row = keep.tile([P, TS_PER_PARTITION], F32, name="ts_row", tag="after_ts_row", align_bytes=64)
-        raw0 = place([P, PACK, NQ], F32, "raw0", at_raw0)
-        raw1 = place([P, PACK, NQ], F32, "raw1", at_raw1)
-        raw_a = place([P, PACK, P], F32, "raw_a", at_raw_a)
-        raw_b = place([P, PACK, P], F32, "raw_b", at_raw_b)
+        raw = [place([P, PACK, NQ], F32, f"raw{o}", o * RAW_BYTES) for o in range(PASSES)]
         pool_words = [keep.tile([P, T], U32, name=f"pool_words{o}") for o in range(PASSES)]
         pool_scales = keep.tile([P, T], U8, name="pool_scales", align_bytes=64)
         ident = keep.tile([P, P], F32, name="ident", tag="after_ident", align_bytes=64)
 
-        def load_q(raw, o, queries):
+        def load_q(o):
             nc.sync.dma_start(
-                out=raw[:],
-                in_=qT[0, o * K_PASS:(o + 1) * K_PASS, queries].rearrange("(p j) w -> p j w", j=PACK),
+                out=raw[o][:],
+                in_=qT[0, o * K_PASS:(o + 1) * K_PASS, :].rearrange("(p j) w -> p j w", j=PACK),
             )
 
         def load_words(o, first, end):
@@ -84,18 +82,17 @@ def tile_attend_sddmm_ts_srt_kernel(tc, qT, k_words, k_scales, ts, offs, out):
         nc.sync.dma_start(out=ts_row[:], in_=ts[0].rearrange("(k m) -> k m", m=TS_PER_PARTITION))
         load_words(0, 0, T)
         nc.sync.dma_start(offsets[:], offs)
-        load_q(raw0, 0, slice(0, NQ))
-        load_q(raw1, 1, slice(0, NQ))
+        load_q(0)
+        load_q(1)
         for quad in range(P // QUADRANT):
             (nc.gpsimd if quad == 0 else nc.sync).dma_start(
                 out=pool_scales[QUADRANT * quad:QUADRANT * quad + SCALE_ROWS * PASSES, :].bitcast(I32),
                 in_=k_scales[:, SCALE_ROWS * quad:SCALE_ROWS * (quad + 1), :].bitcast(I32),
             )
-        load_q(raw_a, LAST, block(0))
+        load_q(LAST)
         load_words(1, 0, T)
         load_words(LAST, 0, reach(HALF))
         load_words(LAST, reach(HALF), T)
-        load_q(raw_b, LAST, block(1))
 
         rows = [keep.tile([P, T], F32, name=f"rows{b}") for b in range(BLOCKS)]
         for b in range(BLOCKS):
@@ -113,83 +110,77 @@ def tile_attend_sddmm_ts_srt_kernel(tc, qT, k_words, k_scales, ts, offs, out):
                 in_=spread[:].rearrange("p m k -> p k m"),
             )
 
+        staged = [keep.tile([P, NQ, PACK], BF16, name=f"staged{o}", tag=tag, align_bytes=64)
+                  for o, tag in enumerate(("after_ts_row", "after_ident", "after_ts_row"))]
         q_codes = [keep.tile([P, NQ], U32, name=f"q_codes{o}", align_bytes=64) for o in range(PASSES)]
         q_scales = [keep.tile([P, NQ], U8, name=f"q_scales{o}", align_bytes=64) for o in range(PASSES)]
-
-        def stage(copy, staged, raw, queries):
-            copy(
-                out=staged[:, queries, :].rearrange("p (c i) j -> p c j i", i=LINE),
-                in_=raw[:, :, queries].rearrange("p j (c i) -> p c j i", i=LINE),
-            )
-
-        def quantize(o, queries, staged):
-            nc.vector.quantize_mx(
-                out=q_codes[o][:, queries].bitcast(FP8X4),
-                scales=q_scales[o][:, queries],
-                in_=staged[:].rearrange("p w j -> p (w j)"),
-            )
-
+        key_words = [keep.tile([P, N], U32, name="key_words0", align_bytes=64),
+                     place([P, N], U32, "key_words1", LAST * RAW_BYTES),
+                     place([P, N], U32, "key_words2", LAST * RAW_BYTES + WORDS_BYTES)]
+        key_scales = place([P, N], U8, "key_scales", 0)
+        ts_listed = keep.tile([P, N], F32, name="ts_listed")
+        scores = [keep.tile([P, N], F32, name=f"scores{b}") for b in range(BLOCKS)]
         acc = {(b, first): psum.tile([P, HALF], F32, name=f"acc{b}_{first}")
                for first in (0, HALF) for b in range(BLOCKS)}
-        scores = [keep.tile([P, N], F32, name=f"scores{b}") for b in range(BLOCKS)]
-        ts_listed = keep.tile([P, N], F32, name="ts_listed")
-        words0 = keep.tile([P, N], U32, name="words0", align_bytes=64)
-        key_words = {(0, first): words0[:, first:first + HALF] for first in (0, HALF)}
 
-        def gather_words(o, first, offset):
-            key_words[o, first] = place([P, HALF], U32, f"words{o}_{first}", offset)[:]
-            nc.vector.tensor_copy(
-                out=key_words[o, first],
-                in_=pool_words[o][:, :reach(first + HALF)].indirect(entries(first, HALF)),
+        def stage(copy, o, queries):
+            copy(
+                out=staged[o][:, queries, :].rearrange("p (c i) j -> p c j i", i=LINE),
+                in_=raw[o][:, :, queries].rearrange("p j (c i) -> p c j i", i=LINE),
             )
 
-        def multiply(o, b, first, stop=False):
+        def quantize(o):
+            nc.vector.quantize_mx(
+                out=q_codes[o][:].bitcast(FP8X4),
+                scales=q_scales[o][:],
+                in_=staged[o][:].rearrange("p w j -> p (w j)"),
+            )
+
+        def gather_words(o, first, slots):
+            nc.vector.tensor_copy(
+                out=key_words[o][:, first:first + slots],
+                in_=pool_words[o][:, :reach(first + slots)].indirect(entries(first, slots)),
+            )
+
+        def multiply(o, b, first):
             nc.tensor.matmul_mx(
                 out=acc[b, first][:],
                 lhsT=q_codes[o][:, block(b)].bitcast(FP8X4),
                 lhsT_scale=q_scales[o][:, block(b)],
-                rhs=key_words[o, first].bitcast(FP8X4),
+                rhs=key_words[o][:, first:first + HALF].bitcast(FP8X4),
                 rhs_scale=key_scales[SCALE_ROWS * o:P, first:first + HALF],
                 start=(o == 0),
-                stop=stop,
+                stop=(o == LAST),
             )
 
-        nc.vector.tensor_copy(out=words0[:], in_=pool_words[0][:].indirect(offsets[:]))
+        gather_words(0, 0, N)
         nc.vector.tensor_copy(out=ts_listed[:], in_=ts_pool[:].indirect(offsets[:]))
-
-        staged0 = keep.tile([P, NQ, PACK], BF16, name="staged0", tag="after_ts_row", align_bytes=64)
-        stage(nc.scalar.copy, staged0, raw0, slice(0, NQ))
-        quantize(0, slice(0, NQ), staged0)
-        key_scales = place([P, N], U8, "key_scales", at_raw0)
+        stage(nc.scalar.copy, 0, slice(0, NQ))
+        quantize(0)
         nc.vector.tensor_copy(out=key_scales[:], in_=pool_scales[:].indirect(offsets[:]))
         for b, first in acc:
             multiply(0, b, first)
 
-        staged1 = keep.tile([P, NQ, PACK], BF16, name="staged1", tag="after_ident", align_bytes=64)
-        stage(nc.scalar.copy, staged1, raw1, slice(0, NQ))
-        quantize(1, slice(0, NQ), staged1)
-        for first in (0, HALF):
-            gather_words(1, first, at_raw1 + 4 * first)
-            for b in range(BLOCKS):
-                multiply(1, b, first)
-
-        at_staged = at_raw0 + HALF_BYTES
-        staged_a = place([P, P, PACK], BF16, "staged_a", at_staged)
-        stage(nc.scalar.copy, staged_a, raw_a, slice(0, P))
-        quantize(LAST, block(0), staged_a)
-        for first in (0, HALF):
-            gather_words(LAST, first, at_raw_a + 4 * first)
-            multiply(LAST, 0, first, stop=True)
-
-        staged_b = place([P, P, PACK], BF16, "staged_b", at_staged)
-        stage(nc.vector.tensor_copy, staged_b, raw_b, slice(0, VECTOR_SHARE))
-        stage(nc.scalar.copy, staged_b, raw_b, slice(VECTOR_SHARE, P))
-        quantize(LAST, block(1), staged_b)
-        for first in (0, HALF):
-            multiply(LAST, 1, first, stop=True)
-
-        for b in range(BLOCKS):
+        stage(nc.scalar.copy, 1, slice(0, NQ))
+        stage(nc.vector.tensor_copy, LAST, slice(0, VECTOR_SHARE))
+        stage(nc.scalar.copy, LAST, slice(VECTOR_SHARE, NQ))
+        quantize(1)
+        quantize(LAST)
+        for o in (1, LAST):
             for first in (0, HALF):
-                nc.scalar.copy(out=scores[b][:, first:first + HALF], in_=acc[b, first][:])
-            nc.vector.tensor_tensor(rows[b][:].indirect(offsets[:]), scores[b][:], ts_listed[:], mybir.AluOpType.mult)
+                gather_words(o, first, HALF)
+                for b in range(BLOCKS):
+                    multiply(o, b, first)
+
+        def weigh_and_scatter(first):
+            half = slice(first, first + HALF)
+            nc.vector.tensor_tensor(scores[0][:, half], acc[0, first][:], ts_listed[:, half], MULT)
+            nc.scalar.activation(rows[0][:].indirect(entries(first, HALF)), scores[0][:, half], COPY)
+
+        weigh_and_scatter(0)
+        for first in (0, HALF):
+            nc.vector.tensor_copy(out=scores[1][:, first:first + HALF], in_=acc[1, first][:])
+        weigh_and_scatter(HALF)
+        nc.vector.tensor_tensor(rows[1][:].indirect(offsets[:]), scores[1][:], ts_listed[:], MULT)
+        for b in range(BLOCKS):
             nc.sync.dma_start(out=out[0, block(b), :], in_=rows[b][:])

@@ -172,15 +172,13 @@ def tile_attend_sddmm_ts_srt_kernel(tc, qT, k_words, k_scales, ts, offs, out):
                 for b in range(BLOCKS):
                     multiply(o, b, first)
 
-        def weigh_and_scatter(first):
-            half = slice(first, first + HALF)
-            nc.vector.tensor_tensor(scores[0][:, half], acc[0, first][:], ts_listed[:, half], MULT)
-            nc.scalar.activation(rows[0][:].indirect(entries(first, HALF)), scores[0][:, half], COPY)
-
-        weigh_and_scatter(0)
-        for first in (0, HALF):
-            nc.vector.tensor_copy(out=scores[1][:, first:first + HALF], in_=acc[1, first][:])
-        weigh_and_scatter(HALF)
-        nc.vector.tensor_tensor(rows[1][:].indirect(offsets[:]), scores[1][:], ts_listed[:], MULT)
+        low, high = slice(0, HALF), slice(HALF, N)
+        nc.vector.tensor_tensor(scores[1][:, low], acc[1, 0][:], ts_listed[:, low], MULT)
+        nc.scalar.copy(out=scores[0][:, low], in_=acc[0, 0][:])
+        nc.scalar.copy(out=scores[0][:, high], in_=acc[0, HALF][:])
+        nc.scalar.activation(rows[1][:].indirect(entries(0, HALF)), scores[1][:, low], COPY)
+        nc.scalar.copy(out=scores[1][:, high], in_=acc[1, HALF][:])
+        nc.vector.tensor_tensor(rows[0][:].indirect(offsets[:]), scores[0][:], ts_listed[:], MULT)
+        nc.vector.tensor_tensor(rows[1][:].indirect(entries(HALF, HALF)), scores[1][:, high], ts_listed[:, high], MULT)
         for b in range(BLOCKS):
             nc.sync.dma_start(out=out[0, block(b), :], in_=rows[b][:])

@@ -28,10 +28,11 @@ LINE = 4
 TS_PER_PARTITION = T // P
 PER_BANK = 4
 
-COPY = mybir.ActivationFunctionType.Copy
 MULT = mybir.AluOpType.mult
 RAW_BYTES = 4 * PACK * NQ
 WORDS_BYTES = 4 * N
+QUARTER = N // 4
+PIECES = ((0, QUARTER), (QUARTER, QUARTER), (HALF, HALF))
 VECTOR_SHARE = 168
 
 
@@ -91,8 +92,8 @@ def tile_attend_sddmm_ts_srt_kernel(tc, qT, k_words, k_scales, ts, offs, out):
             )
         load_q(LAST)
         load_words(1, 0, T)
-        load_words(LAST, 0, reach(HALF))
-        load_words(LAST, reach(HALF), T)
+        for first, slots in PIECES:
+            load_words(LAST, reach(first) if first else 0, reach(first + slots))
 
         rows = [keep.tile([P, T], F32, name=f"rows{b}") for b in range(BLOCKS)]
         for b in range(BLOCKS):
@@ -120,8 +121,10 @@ def tile_attend_sddmm_ts_srt_kernel(tc, qT, k_words, k_scales, ts, offs, out):
         key_scales = place([P, N], U8, "key_scales", 0)
         ts_listed = keep.tile([P, N], F32, name="ts_listed")
         scores = [keep.tile([P, N], F32, name=f"scores{b}") for b in range(BLOCKS)]
-        acc = {(b, first): psum.tile([P, HALF], F32, name=f"acc{b}_{first}")
-               for first in (0, HALF) for b in range(BLOCKS)}
+        acc = {(0, first): psum.tile([P, slots], F32, name=f"acc0_{first}")[:] for first, slots in PIECES}
+        acc[1, 0] = psum.tile([P, QUARTER], F32, name="acc1_0")[:]
+        late = psum.tile([P, N - QUARTER], F32, name="acc1_late")
+        acc[1, QUARTER], acc[1, HALF] = late[:, :QUARTER], late[:, QUARTER:]
 
         def stage(copy, o, queries):
             copy(
@@ -142,43 +145,61 @@ def tile_attend_sddmm_ts_srt_kernel(tc, qT, k_words, k_scales, ts, offs, out):
                 in_=pool_words[o][:, :reach(first + slots)].indirect(entries(first, slots)),
             )
 
-        def multiply(o, b, first):
+        def multiply(o, b, piece):
+            first, slots = PIECES[piece]
             nc.tensor.matmul_mx(
-                out=acc[b, first][:],
+                out=acc[b, first],
                 lhsT=q_codes[o][:, block(b)].bitcast(FP8X4),
                 lhsT_scale=q_scales[o][:, block(b)],
-                rhs=key_words[o][:, first:first + HALF].bitcast(FP8X4),
-                rhs_scale=key_scales[SCALE_ROWS * o:P, first:first + HALF],
-                start=(o == 0),
-                stop=(o == LAST),
+                rhs=key_words[o][:, first:first + slots].bitcast(FP8X4),
+                rhs_scale=key_scales[SCALE_ROWS * o:P, first:first + slots],
+                start=(o == 0 and (b, first) != (1, HALF)),
+                stop=(o == LAST and (b, first) != (1, QUARTER)),
             )
+
+        def scatter(b, first, end):
+            nc.vector.tensor_tensor(rows[b][:].indirect(entries(first, end - first)), scores[b][:, first:end],
+                                    ts_listed[:, first:end], MULT)
 
         gather_words(0, 0, N)
         nc.vector.tensor_copy(out=ts_listed[:], in_=ts_pool[:].indirect(offsets[:]))
         stage(nc.scalar.copy, 0, slice(0, NQ))
         quantize(0)
         nc.vector.tensor_copy(out=key_scales[:], in_=pool_scales[:].indirect(offsets[:]))
-        for b, first in acc:
-            multiply(0, b, first)
+        for b in range(BLOCKS):
+            for piece in range(len(PIECES)):
+                multiply(0, b, piece)
 
         stage(nc.scalar.copy, 1, slice(0, NQ))
         stage(nc.vector.tensor_copy, LAST, slice(0, VECTOR_SHARE))
         stage(nc.scalar.copy, LAST, slice(VECTOR_SHARE, NQ))
         quantize(1)
         quantize(LAST)
-        for o in (1, LAST):
-            for first in (0, HALF):
-                gather_words(o, first, HALF)
-                for b in range(BLOCKS):
-                    multiply(o, b, first)
+        for first in (0, HALF):
+            gather_words(1, first, HALF)
+        for first, slots in PIECES:
+            gather_words(LAST, first, slots)
 
-        low, high = slice(0, HALF), slice(HALF, N)
-        nc.vector.tensor_tensor(scores[1][:, low], acc[1, 0][:], ts_listed[:, low], MULT)
-        nc.scalar.copy(out=scores[0][:, low], in_=acc[0, 0][:])
-        nc.scalar.copy(out=scores[0][:, high], in_=acc[0, HALF][:])
-        nc.scalar.activation(rows[1][:].indirect(entries(0, HALF)), scores[1][:, low], COPY)
-        nc.scalar.copy(out=scores[1][:, high], in_=acc[1, HALF][:])
-        nc.vector.tensor_tensor(rows[0][:].indirect(offsets[:]), scores[0][:], ts_listed[:], MULT)
-        nc.vector.tensor_tensor(rows[1][:].indirect(entries(HALF, HALF)), scores[1][:, high], ts_listed[:, high], MULT)
+        multiply(1, 0, 0)
+        multiply(1, 1, 0)
+        multiply(1, 0, 1)
+        multiply(1, 0, 2)
+        multiply(LAST, 0, 0)
+        multiply(LAST, 1, 0)
+        multiply(LAST, 0, 1)
+        multiply(1, 1, 1)
+        multiply(LAST, 0, 2)
+        multiply(1, 1, 2)
+        multiply(LAST, 1, 1)
+        multiply(LAST, 1, 2)
+
+        for b in range(BLOCKS):
+            nc.scalar.copy(out=scores[b][:, :QUARTER], in_=acc[b, 0])
+        for first, slots in PIECES[1:]:
+            nc.scalar.copy(out=scores[0][:, first:first + slots], in_=acc[0, first])
+        nc.scalar.copy(out=scores[1][:, QUARTER:], in_=late[:])
+        for first, end in ((0, QUARTER), (QUARTER, N)):
+            for b in range(BLOCKS):
+                scatter(b, first, end)
         for b in range(BLOCKS):
             nc.sync.dma_start(out=out[0, block(b), :], in_=rows[b][:])

from contextlib import ExitStack

import concourse.mybir as mybir
from concourse.masks import make_identity

NQ, N, T, D = 256, 512, 1024, 1536
FLOPS = 2 * NQ * N * D

F32 = mybir.dt.float32
BF16 = mybir.dt.bfloat16
I32 = mybir.dt.int32
U32 = mybir.dt.uint32
U16 = mybir.dt.uint16
U8 = mybir.dt.uint8
FP8X4 = mybir.dt.float8_e4m3fn_x4

P = 128
PACK = 4
K_PASS = P * PACK
PASSES = D // K_PASS
LAST = PASSES - 1
QUADRANT = 32
SCALE_ROWS = 4
PER_COLUMN = 16
BLOCKS = NQ // P
HALF = N // 2
LINE = 4
TS_PER_PARTITION = T // P
PER_BANK = 4

MULT = mybir.AluOpType.mult
RAW_BYTES = 4 * PACK * NQ
WORDS_BYTES = 4 * N
QUARTER = N // 4
PIECES = ((0, QUARTER), (QUARTER, QUARTER), (HALF, HALF))
VECTOR_SHARE = 168


def block(b):
    return slice(b * P, (b + 1) * P)


def reach(end_slot):
    return T - (N - end_slot)


def tile_attend_sddmm_ts_srt_kernel(tc, qT, k_words, k_scales, ts, offs, out):
    nc = tc.nc
    with ExitStack() as ctx:
        keep = ctx.enter_context(tc.tile_pool(name="keep", bufs=1))
        placed = ctx.enter_context(tc.tile_pool(name="placed", bufs=1))
        psum = ctx.enter_context(tc.psum_pool(name="psum", bufs=1))

        def place(shape, dtype, name, offset):
            return placed.tile(shape, dtype, name=name, align_bytes=64, offset=offset)

        offsets = keep.tile([P, N // PER_COLUMN], U16, name="offsets")
        ts_row = keep.tile([P, TS_PER_PARTITION], F32, name="ts_row", tag="after_ts_row", align_bytes=64)
        raw = [place([P, PACK, NQ], F32, f"raw{o}", o * RAW_BYTES) for o in range(PASSES)]
        pool_words = [keep.tile([P, T], U32, name=f"pool_words{o}") for o in range(PASSES)]
        pool_scales = keep.tile([P, T], U8, name="pool_scales", align_bytes=64)
        ident = keep.tile([P, P], F32, name="ident", tag="after_ident", align_bytes=64)

        def load_q(o):
            nc.sync.dma_start(
                out=raw[o][:],
                in_=qT[0, o * K_PASS:(o + 1) * K_PASS, :].rearrange("(p j) w -> p j w", j=PACK),
            )

        def load_words(o, first, end):
            nc.sync.dma_start(
                out=pool_words[o][:, first:end].bitcast(I32),
                in_=k_words[o, :, first:end, :].rearrange("p t r -> p (t r)").bitcast(I32),
            )

        def entries(first_slot, slots):
            return offsets[:, first_slot // PER_COLUMN:(first_slot + slots) // PER_COLUMN]

        nc.vector.memset(ident[:], 0.0)
        nc.vector.memset(pool_scales[:].bitcast(I32), 0)
        make_identity(nc, ident[:], nomemset=True)

        nc.sync.dma_start(out=ts_row[:], in_=ts[0].rearrange("(k m) -> k m", m=TS_PER_PARTITION))
        load_words(0, 0, T)
        nc.sync.dma_start(offsets[:], offs)
        load_q(0)
        load_q(1)
        for quad in range(P // QUADRANT):
            (nc.gpsimd if quad == 0 else nc.sync).dma_start(
                out=pool_scales[QUADRANT * quad:QUADRANT * quad + SCALE_ROWS * PASSES, :].bitcast(I32),
                in_=k_scales[:, SCALE_ROWS * quad:SCALE_ROWS * (quad + 1), :].bitcast(I32),
            )
        load_q(LAST)
        load_words(1, 0, T)
        for first, slots in PIECES:
            load_words(LAST, reach(first) if first else 0, reach(first + slots))

        rows = [keep.tile([P, T], F32, name=f"rows{b}") for b in range(BLOCKS)]
        for b in range(BLOCKS):
            nc.vector.memset(rows[b][:], 0.0)

        ts_pool = keep.tile([P, T], F32, name="ts_pool")
        banks = TS_PER_PARTITION // PER_BANK
        for g in range(banks):
            spread = psum.tile([P, PER_BANK, P], F32, name=f"spread{g}")
            for m in range(PER_BANK):
                col = PER_BANK * g + m
                nc.tensor.transpose(spread[:, m, :], ts_row[:, col:col + 1].to_broadcast([P, P]), ident[:])
            nc.scalar.copy(
                out=ts_pool[:].rearrange("p (k g m) -> p k g m", g=banks, m=PER_BANK)[:, :, g, :],
                in_=spread[:].rearrange("p m k -> p k m"),
            )

        staged = [keep.tile([P, NQ, PACK], BF16, name=f"staged{o}", tag=tag, align_bytes=64)
                  for o, tag in enumerate(("after_ts_row", "after_ident", "after_ts_row"))]
        q_codes = [keep.tile([P, NQ], U32, name=f"q_codes{o}", align_bytes=64) for o in range(PASSES)]
        q_scales = [keep.tile([P, NQ], U8, name=f"q_scales{o}", align_bytes=64) for o in range(PASSES)]
        key_words = [keep.tile([P, N], U32, name="key_words0", align_bytes=64),
                     place([P, N], U32, "key_words1", LAST * RAW_BYTES),
                     place([P, N], U32, "key_words2", LAST * RAW_BYTES + WORDS_BYTES)]
        key_scales = place([P, N], U8, "key_scales", 0)
        ts_listed = keep.tile([P, N], F32, name="ts_listed")
        scores = [keep.tile([P, N], F32, name=f"scores{b}") for b in range(BLOCKS)]
        acc = {(0, first): psum.tile([P, slots], F32, name=f"acc0_{first}")[:] for first, slots in PIECES}
        acc[1, 0] = psum.tile([P, QUARTER], F32, name="acc1_0")[:]
        late = psum.tile([P, N - QUARTER], F32, name="acc1_late")
        acc[1, QUARTER], acc[1, HALF] = late[:, :QUARTER], late[:, QUARTER:]

        def stage(copy, o, queries):
            copy(
                out=staged[o][:, queries, :].rearrange("p (c i) j -> p c j i", i=LINE),
                in_=raw[o][:, :, queries].rearrange("p j (c i) -> p c j i", i=LINE),
            )

        def quantize(o):
            nc.vector.quantize_mx(
                out=q_codes[o][:].bitcast(FP8X4),
                scales=q_scales[o][:],
                in_=staged[o][:].rearrange("p w j -> p (w j)"),
            )

        def gather_words(o, first, slots):
            nc.vector.tensor_copy(
                out=key_words[o][:, first:first + slots],
                in_=pool_words[o][:, :reach(first + slots)].indirect(entries(first, slots)),
            )

        def multiply(o, b, piece):
            first, slots = PIECES[piece]
            nc.tensor.matmul_mx(
                out=acc[b, first],
                lhsT=q_codes[o][:, block(b)].bitcast(FP8X4),
                lhsT_scale=q_scales[o][:, block(b)],
                rhs=key_words[o][:, first:first + slots].bitcast(FP8X4),
                rhs_scale=key_scales[SCALE_ROWS * o:P, first:first + slots],
                start=(o == 0 and (b, first) != (1, HALF)),
                stop=(o == LAST and (b, first) != (1, QUARTER)),
            )

        def scatter(b, first, end):
            nc.vector.tensor_tensor(rows[b][:].indirect(entries(first, end - first)), scores[b][:, first:end],
                                    ts_listed[:, first:end], MULT)

        gather_words(0, 0, N)
        nc.vector.tensor_copy(out=ts_listed[:], in_=ts_pool[:].indirect(offsets[:]))
        stage(nc.scalar.copy, 0, slice(0, NQ))
        quantize(0)
        nc.vector.tensor_copy(out=key_scales[:], in_=pool_scales[:].indirect(offsets[:]))
        for b in range(BLOCKS):
            for piece in range(len(PIECES)):
                multiply(0, b, piece)

        stage(nc.scalar.copy, 1, slice(0, NQ))
        stage(nc.vector.tensor_copy, LAST, slice(0, VECTOR_SHARE))
        stage(nc.scalar.copy, LAST, slice(VECTOR_SHARE, NQ))
        quantize(1)
        quantize(LAST)
        for first in (0, HALF):
            gather_words(1, first, HALF)
        for first, slots in PIECES:
            gather_words(LAST, first, slots)

        multiply(1, 0, 0)
        multiply(1, 1, 0)
        multiply(1, 0, 1)
        multiply(1, 0, 2)
        multiply(LAST, 0, 0)
        multiply(LAST, 1, 0)
        multiply(LAST, 0, 1)
        multiply(1, 1, 1)
        multiply(LAST, 0, 2)
        multiply(1, 1, 2)
        multiply(LAST, 1, 1)
        multiply(LAST, 1, 2)

        for b in range(BLOCKS):
            nc.scalar.copy(out=scores[b][:, :QUARTER], in_=acc[b, 0])
        for first, slots in PIECES[1:]:
            nc.scalar.copy(out=scores[0][:, first:first + slots], in_=acc[0, first])
        nc.scalar.copy(out=scores[1][:, QUARTER:], in_=late[:])
        for first, end in ((0, QUARTER), (QUARTER, N)):
            for b in range(BLOCKS):
                scatter(b, first, end)
        for b in range(BLOCKS):
            nc.sync.dma_start(out=out[0, block(b), :], in_=rows[b][:])
